import numpy as np
import ml_dtypes


def mxq(x, axis, fmt="e4m3"):
    dtype, down = {"e4m3": (ml_dtypes.float8_e4m3fn, 7), "e5m2": (ml_dtypes.float8_e5m2, 14)}[fmt]
    v = np.moveaxis(np.asarray(x, np.float32).astype(ml_dtypes.bfloat16).astype(np.float64), axis, -1)
    blocks = v.reshape(v.shape[:-1] + (-1, 32))
    amax = np.abs(blocks).max(-1, keepdims=True)
    byte = np.maximum(np.where(amax > 0, np.frexp(amax)[1] - 1 + 127, 0) - down, 1)
    scale = np.exp2(byte - 127.0)
    codes = (blocks / scale).astype(np.float32).astype(dtype).astype(np.float64)
    return np.moveaxis((codes * scale).reshape(v.shape), -1, axis)


WIDE = False


def mx_kscale(k):
    if not WIDE:
        return np.ones(k)
    levels = np.array([10, -10, 5, -5, 0])
    if k % 512:
        return np.exp2(np.random.permutation(np.resize(levels, k // 32))).repeat(32)
    a = np.empty((k // 512, 16))
    for p in range(k // 512):
        a[p, :8] = np.random.permutation(np.resize(levels, 8))
        for g in range(8):
            far = levels[np.abs(levels - a[p, g]) >= 10]
            a[p, g + 8] = far[np.random.randint(len(far))]
    return np.exp2(a.ravel()).repeat(32)


def f64(x):
    return np.asarray(x).astype(np.float64)


def striped(idx):
    return np.tile(idx.reshape(-1, 16).T, (8, 1)).astype(np.uint16)


def unstriped(offs):
    return offs[:16].T.reshape(-1).astype(np.int64)


def pack_weight(w):
    k, n = w.shape
    w = f64(np.asarray(w, np.float32).astype(ml_dtypes.bfloat16)).reshape(k // 32, 32, n)
    amax = np.abs(w).max(1)
    byte = np.clip(np.where(amax > 0, np.frexp(amax)[1] - 1 + 127 - 7, 1), 1, 254)
    scaled = (w * np.exp2(127.0 - byte)[:, None, :]).reshape(k, n).astype(np.float32)
    words = np.ascontiguousarray(scaled.reshape(k // 512, 128, 4, n).transpose(0, 1, 3, 2)).astype(ml_dtypes.float8_e4m3fn).view(np.uint8)
    return words, np.ascontiguousarray(byte.astype(np.uint8).reshape(k // 512, 16, n))


def unpack_weight(words, scales):
    g, p, n, _ = words.shape
    vals = np.ascontiguousarray(words).view(ml_dtypes.float8_e4m3fn).astype(np.float64) * np.repeat(np.exp2(scales.astype(np.float64) - 127.0), 8, axis=1)[..., None]
    return vals.transpose(0, 1, 3, 2).reshape(g * 512, n)


def planes(y):
    n, m = y.shape
    v = y.astype(np.float32).astype(ml_dtypes.bfloat16).astype(np.float64).reshape(n // 32, 32, m)
    top = np.abs(v).max(1)
    byte = np.clip(np.where(top > 0, np.frexp(top)[1] - 1 + 127 - 7, 1), 1, 254)
    codes = (v * np.exp2(127.0 - byte)[:, None, :]).reshape(n, m).astype(np.float32).astype(ml_dtypes.float8_e4m3fn).view(np.uint8)
    words = codes.reshape(n // 512, 128, 4, m).transpose(0, 1, 3, 2)
    return np.ascontiguousarray(words), np.ascontiguousarray(byte.astype(np.uint8).reshape(n // 512, 16, m))


K, T, S, H, N = 512, 2048, 512, 512, 512


def setup_inputs():
    n = np.random.standard_normal
    s = mx_kscale(K)[:, None]
    u = mx_kscale(H)
    packed_xT = pack_weight(n((K, T)) * s)
    return {
        "x_words": packed_xT[0],
        "x_scales": packed_xT[1],
        "w1": (n((K, H)) / np.sqrt(K) / s * u).astype(np.float32),
        "w2": (n((H, N)) / np.sqrt(H) / u[:, None]).astype(np.float32),
        "eq": (n((H, S)) * u[:, None]).astype(np.float32),
        "rate": (np.random.uniform(0.2, 1.8, (H, 1))).astype(np.float32),
        "offs": striped(np.random.permutation(T)[:S]),
        "src": striped(np.random.permutation(S)),
    }


def reference(x_words, x_scales, w1, w2, eq, rate, offs, src):
    xq = unpack_weight(x_words, x_scales)[:, unstriped(offs)]
    y = mxq(f64(w1), 0, "e4m3").T @ xq
    rr = y + f64(rate) * (f64(eq) - y)
    f = mxq(f64(w2), 0, "e4m3").T @ mxq(rr, 0, "e4m3")
    out_0 = f[:, unstriped(src)]
    return (out_0,) + planes(out_0)

@@ -1,0 +1,214 @@
+from contextlib import ExitStack
+
+import concourse.mybir as mybir
+
+K, T, S, H, N = 512, 2048, 512, 512, 512
+FLOPS = 2 * K * H * S + 2 * H * N * S
+
+F32 = mybir.dt.float32
+BF16 = mybir.dt.bfloat16
+I32 = mybir.dt.int32
+U32 = mybir.dt.uint32
+U16 = mybir.dt.uint16
+U8 = mybir.dt.uint8
+FP8X4 = mybir.dt.float8_e4m3fn_x4
+ALU = mybir.AluOpType
+ACT = mybir.ActivationFunctionType
+
+P = 128
+PACK = 4
+HALF = 256
+QUARTER = 128
+
+
+def tile_picked_ylbm_str_po_kernel(
+    tc, x_words, x_scales, w1, w2, eq, rate, offs, src, out_0, out_1, out_2
+):
+    nc = tc.nc
+    with ExitStack() as ctx:
+        sb = ctx.enter_context(tc.tile_pool(name="sb", bufs=1))
+        psum = ctx.enter_context(tc.psum_pool(name="psum", bufs=1))
+
+        def tile(shape, dtype, name, tag=None):
+            return sb.tile(shape, dtype, name=name, tag=tag or name, align_bytes=64)
+
+        offs_sb = tile([P, S // 16], U16, "offs_sb")
+        src_sb = tile([P, S // 16], U16, "src_sb")
+        xs_table = tile([P, T], U8, "xs_table")
+        xw_table = tile([P, T], I32, "xw_table")
+        rate_sb = tile([P, PACK], F32, "rate_sb")
+        keep_sb = tile([P, PACK], F32, "keep_sb")
+
+        def load_halves(dram, name, tags):
+            rows = dram.rearrange("(p j) c -> p j c", j=PACK)
+            halves = []
+            for h in range(2):
+                raw = tile([P, PACK, HALF], F32, name + str(h), tags[h])
+                nc.sync.dma_start(out=raw[:], in_=rows[:, :, h * HALF : (h + 1) * HALF])
+                halves.append(raw)
+            return halves
+
+        nc.vector.memset(xs_table[:].bitcast(I32), 0)
+        nc.sync.dma_start(offs_sb[:], offs)
+        for q in range(4):
+            nc.scalar.dma_start(
+                out=xs_table[32 * q : 32 * q + 4, :].bitcast(I32),
+                in_=x_scales[0, 4 * q : 4 * q + 4, :].bitcast(I32),
+            )
+        nc.scalar.dma_start(out=rate_sb[:], in_=rate.rearrange("(p t) o -> p (t o)", t=PACK))
+        w1_raw = load_halves(w1, "w1_raw", ("raw0", "raw1"))
+        nc.sync.dma_start(out=xw_table[:], in_=x_words[0].rearrange("p n t -> p (n t)").bitcast(I32))
+        nc.sync.dma_start(src_sb[:], src)
+
+        def deal_weights(copy, grouped, raw, h):
+            m = HALF // PACK
+            copy(
+                out=grouped[:, :, h * m : (h + 1) * m, :].rearrange("p t m j -> p m j t"),
+                in_=raw[:].rearrange("p j (m t) -> p m j t", t=PACK),
+            )
+
+        def quantize_weights(grouped, name):
+            made = []
+            for t in range(PACK):
+                codes = tile([P, P], I32, name + "_codes" + str(t))
+                scales = tile([P, P], U8, name + "_scales" + str(t))
+                nc.vector.quantize_mx(
+                    out=codes[:].bitcast(FP8X4),
+                    scales=scales[:],
+                    in_=grouped[:, t, :, :].rearrange("p m j -> p (m j)"),
+                )
+                made.append((codes, scales))
+            return made
+
+        def product(bank, weights, codes, scales):
+            nc.tensor.matmul_mx(
+                out=bank[:],
+                lhsT=weights[0][:].bitcast(FP8X4),
+                lhsT_scale=weights[1][:],
+                rhs=codes.bitcast(FP8X4),
+                rhs_scale=scales,
+                start=True,
+                stop=True,
+            )
+
+        nc.vector.tensor_scalar(keep_sb[:], rate_sb[:], -1.0, 1.0, ALU.mult, ALU.add)
+
+        x_scale = []
+        for h in range(2):
+            picked = tile([P, HALF], U8, "x_scale" + str(h))
+            nc.vector.tensor_copy(picked[:], xs_table[:].indirect(offs_sb[:, 16 * h : 16 * (h + 1)]))
+            x_scale.append(picked)
+
+        w1_grouped = tile([P, PACK, P, PACK], BF16, "w1_grouped")
+        deal_weights(nc.scalar.copy, w1_grouped, w1_raw[0], 0)
+        deal_weights(nc.vector.tensor_copy, w1_grouped, w1_raw[1], 1)
+        w1_mx = quantize_weights(w1_grouped, "w1")
+        eq_raw = load_halves(eq, "eq_raw", ("raw0", "raw1"))
+
+        x_word = []
+        for h in range(2):
+            picked = tile([P, HALF], I32, "x_word" + str(h))
+            nc.vector.tensor_copy(
+                picked[:].bitcast(U32),
+                xw_table[:].bitcast(U32).indirect(offs_sb[:, 16 * h : 16 * (h + 1)]),
+            )
+            x_word.append(picked)
+
+        w2_raw = load_halves(w2, "w2_raw", ("w1_grouped", "xw_table"))
+
+        kept = []
+        for h in range(2):
+            z = tile([P, PACK, HALF], F32, "kept" + str(h))
+            for t in range(PACK):
+                bank = psum.tile([P, HALF], F32, name="bank%d%d" % (h, t))
+                product(bank, w1_mx[t], x_word[h][:], x_scale[h][:])
+                if (h, t) == (0, PACK - 1):
+                    nc.vector.tensor_scalar(z[:, t, :], bank[:], keep_sb[:, t : t + 1], None, ALU.mult)
+                else:
+                    nc.scalar.activation(z[:, t, :], bank[:], ACT.Copy, scale=keep_sb[:, t : t + 1])
+            kept.append(z)
+
+        rr_halves = []
+        for h in range(2):
+            pull = tile([P, PACK, HALF], F32, "pull" + str(h))
+            for t in range(PACK):
+                nc.vector.tensor_scalar(pull[:, t, :], eq_raw[h][:, t, :], rate_sb[:, t : t + 1], None, ALU.mult)
+            rr = tile([P, HALF, PACK], BF16, "rr" + str(h))
+            nc.vector.tensor_tensor(
+                rr[:].rearrange("p (c i) t -> p c t i", i=4),
+                kept[h][:].rearrange("p t (c i) -> p c t i", i=4),
+                pull[:].rearrange("p t (c i) -> p c t i", i=4),
+                ALU.add,
+            )
+            rr_halves.append(rr)
+        rr_codes = tile([P, S], I32, "rr_codes")
+        rr_scales = tile([P, S], U8, "rr_scales")
+        for h in range(2):
+            cols = slice(h * HALF, (h + 1) * HALF)
+            nc.vector.quantize_mx(
+                out=rr_codes[:, cols].bitcast(FP8X4),
+                scales=rr_scales[:, cols],
+                in_=rr_halves[h][:].rearrange("p n t -> p (n t)"),
+            )
+
+        w2_grouped = tile([P, PACK, P, PACK], BF16, "w2_grouped")
+        deal_weights(nc.scalar.copy, w2_grouped, w2_raw[0], 0)
+        deal_weights(nc.scalar.copy, w2_grouped, w2_raw[1], 1)
+        w2_mx = quantize_weights(w2_grouped, "w2")
+
+        f_rows = tile([P, PACK * S], F32, "f_rows")
+        for t in range(PACK):
+            width = HALF if t == 0 else S
+            for h in range(S // width):
+                cols = slice(h * width, (h + 1) * width)
+                bank = psum.tile([P, width], F32, name="bank%d%d" % (h, t))
+                product(bank, w2_mx[t], rr_codes[:, cols], rr_scales[:, cols])
+                nc.scalar.copy(out=f_rows[:, t * S + cols.start : t * S + cols.stop], in_=bank[:])
+
+        out_rows = out_0.rearrange("(p t) n -> p t n", t=PACK)
+        out_words = out_1[0].rearrange("p n t -> p (n t)").bitcast(I32)
+        out_scales = tile([P, S], U8, "out_scales")
+        streamed = [tile([P, PACK, HALF], F32, "streamed" + str(h)) for h in range(2)]
+
+        def stream(t, first, width, window_end):
+            h, at = divmod(first, HALF)
+            nc.vector.tensor_copy(
+                streamed[h][:, t, at : at + width],
+                f_rows[:, t * S : window_end].indirect(src_sb[:, first // 16 : (first + width) // 16]),
+            )
+
+        def hand_out(first, width, copy):
+            h, at = divmod(first, HALF)
+            cols = slice(first, first + width)
+            values = streamed[h][:, :, at : at + width]
+            nc.sync.dma_start(out=out_rows[:, :, cols], in_=values)
+            rounded = tile([P, width, PACK], BF16, "rounded" + str(first))
+            copy(
+                out=rounded[:].rearrange("p (c i) t -> p c t i", i=4),
+                in_=values.rearrange("p t (c i) -> p c t i", i=4),
+            )
+            codes = tile([P, width], I32, "out_codes" + str(first))
+            nc.vector.quantize_mx(
+                out=codes[:].bitcast(FP8X4),
+                scales=out_scales[:, cols],
+                in_=rounded[:].rearrange("p n t -> p (n t)"),
+            )
+            nc.sync.dma_start(out=out_words[:, cols], in_=codes[:])
+
+        for t in range(PACK):
+            stream(t, 0, HALF, (t + 1) * S)
+        for t in range(2):
+            stream(t, HALF, HALF, PACK * S)
+        for t in range(2, PACK):
+            stream(t, HALF, QUARTER, PACK * S)
+        hand_out(0, HALF, nc.scalar.copy)
+        for t in range(2, PACK):
+            stream(t, HALF + QUARTER, QUARTER, PACK * S)
+        hand_out(HALF, QUARTER, nc.scalar.copy)
+        hand_out(HALF + QUARTER, QUARTER, nc.vector.tensor_copy)
+        for q in range(4):
+            queue = nc.sync if q % 2 else nc.scalar
+            queue.dma_start(
+                out=out_2[0, 4 * q : 4 * q + 4, :].bitcast(I32),
+                in_=out_scales[32 * q : 32 * q + 4, :].bitcast(I32),
+            )

@@ -19,6 +19,7 @@ P = 128
 PACK = 4
 HALF = 256
 QUARTER = 128
+PIECES = (slice(0, HALF), slice(HALF, HALF + QUARTER), slice(HALF + QUARTER, 2 * HALF))
 
 
 def tile_picked_ylbm_str_po_kernel(
@@ -39,14 +40,12 @@ def tile_picked_ylbm_str_po_kernel(
         rate_sb = tile([P, PACK], F32, "rate_sb")
         keep_sb = tile([P, PACK], F32, "keep_sb")
 
-        def load_halves(dram, name, tags):
+        def load_half(dram, h, raw, step=PACK):
             rows = dram.rearrange("(p j) c -> p j c", j=PACK)
-            halves = []
-            for h in range(2):
-                raw = tile([P, PACK, HALF], F32, name + str(h), tags[h])
-                nc.sync.dma_start(out=raw[:], in_=rows[:, :, h * HALF : (h + 1) * HALF])
-                halves.append(raw)
-            return halves
+            raw = raw.rearrange("p (j c) -> p j c", j=PACK)
+            for j in range(0, PACK, step):
+                nc.sync.dma_start(out=raw[:, j : j + step, :], in_=rows[:, j : j + step, h * HALF : (h + 1) * HALF])
+            return raw
 
         nc.vector.memset(xs_table[:].bitcast(I32), 0)
         nc.sync.dma_start(offs_sb[:], offs)
@@ -56,7 +55,7 @@ def tile_picked_ylbm_str_po_kernel(
                 in_=x_scales[0, 4 * q : 4 * q + 4, :].bitcast(I32),
             )
         nc.scalar.dma_start(out=rate_sb[:], in_=rate.rearrange("(p t) o -> p (t o)", t=PACK))
-        w1_raw = load_halves(w1, "w1_raw", ("raw0", "raw1"))
+        w1_raw = [load_half(w1, h, tile([P, PACK * HALF], F32, "w1_raw" + str(h))[:]) for h in range(2)]
         nc.sync.dma_start(out=xw_table[:], in_=x_words[0].rearrange("p n t -> p (n t)").bitcast(I32))
         nc.sync.dma_start(src_sb[:], src)
 
@@ -64,21 +63,18 @@ def tile_picked_ylbm_str_po_kernel(
             m = HALF // PACK
             copy(
                 out=grouped[:, :, h * m : (h + 1) * m, :].rearrange("p t m j -> p m j t"),
-                in_=raw[:].rearrange("p j (m t) -> p m j t", t=PACK),
+                in_=raw.rearrange("p j (m t) -> p m j t", t=PACK),
             )
 
-        def quantize_weights(grouped, name):
-            made = []
-            for t in range(PACK):
-                codes = tile([P, P], I32, name + "_codes" + str(t))
-                scales = tile([P, P], U8, name + "_scales" + str(t))
-                nc.vector.quantize_mx(
-                    out=codes[:].bitcast(FP8X4),
-                    scales=scales[:],
-                    in_=grouped[:, t, :, :].rearrange("p m j -> p (m j)"),
-                )
-                made.append((codes, scales))
-            return made
+        def quantize_weights(grouped, name, t):
+            codes = tile([P, P], I32, name + "_codes" + str(t))
+            scales = tile([P, P], U8, name + "_scales" + str(t))
+            nc.vector.quantize_mx(
+                out=codes[:].bitcast(FP8X4),
+                scales=scales[:],
+                in_=grouped[:, t, :, :].rearrange("p m j -> p (m j)"),
+            )
+            return codes, scales
 
         def product(bank, weights, codes, scales):
             nc.tensor.matmul_mx(
@@ -101,9 +97,12 @@ def tile_picked_ylbm_str_po_kernel(
 
         w1_grouped = tile([P, PACK, P, PACK], BF16, "w1_grouped")
         deal_weights(nc.scalar.copy, w1_grouped, w1_raw[0], 0)
+        late = tile([P, 4 * PACK * HALF], F32, "late", "w1_raw0")
+        parts = [late[:, i * PACK * HALF : (i + 1) * PACK * HALF] for i in range(4)]
+        eq_raw = [load_half(eq, 0, parts[0], 2), load_half(eq, 1, parts[1])]
+        w2_raw = [load_half(w2, h, parts[2 + h]) for h in range(2)]
         deal_weights(nc.vector.tensor_copy, w1_grouped, w1_raw[1], 1)
-        w1_mx = quantize_weights(w1_grouped, "w1")
-        eq_raw = load_halves(eq, "eq_raw", ("raw0", "raw1"))
+        w1_mx = [quantize_weights(w1_grouped, "w1", t) for t in range(PACK)]
 
         x_word = []
         for h in range(2):
@@ -114,56 +113,58 @@ def tile_picked_ylbm_str_po_kernel(
             )
             x_word.append(picked)
 
-        w2_raw = load_halves(w2, "w2_raw", ("w1_grouped", "xw_table"))
 
-        kept = []
-        for h in range(2):
-            z = tile([P, PACK, HALF], F32, "kept" + str(h))
-            for t in range(PACK):
-                bank = psum.tile([P, HALF], F32, name="bank%d%d" % (h, t))
-                product(bank, w1_mx[t], x_word[h][:], x_scale[h][:])
-                if (h, t) == (0, PACK - 1):
-                    nc.vector.tensor_scalar(z[:, t, :], bank[:], keep_sb[:, t : t + 1], None, ALU.mult)
-                else:
-                    nc.scalar.activation(z[:, t, :], bank[:], ACT.Copy, scale=keep_sb[:, t : t + 1])
-            kept.append(z)
-
-        rr_halves = []
+        rr_rows = []
         for h in range(2):
             pull = tile([P, PACK, HALF], F32, "pull" + str(h))
+            rows = tile([P, PACK, HALF], BF16, "rr_rows" + str(h))
             for t in range(PACK):
-                nc.vector.tensor_scalar(pull[:, t, :], eq_raw[h][:, t, :], rate_sb[:, t : t + 1], None, ALU.mult)
-            rr = tile([P, HALF, PACK], BF16, "rr" + str(h))
-            nc.vector.tensor_tensor(
-                rr[:].rearrange("p (c i) t -> p c t i", i=4),
-                kept[h][:].rearrange("p t (c i) -> p c t i", i=4),
-                pull[:].rearrange("p t (c i) -> p c t i", i=4),
-                ALU.add,
-            )
-            rr_halves.append(rr)
+                nc.scalar.activation(pull[:, t, :], eq_raw[h][:, t, :], ACT.Copy, scale=rate_sb[:, t : t + 1])
+                bank = psum.tile([P, HALF], F32, name="bank" + str(PACK * h + t))
+                product(bank, w1_mx[t], x_word[h][:], x_scale[h][:])
+                nc.vector.scalar_tensor_tensor(
+                    rows[:, t, :], bank[:], keep_sb[:, t : t + 1], pull[:, t, :], ALU.mult, ALU.add
+                )
+            rr_rows.append(rows)
+
         rr_codes = tile([P, S], I32, "rr_codes")
         rr_scales = tile([P, S], U8, "rr_scales")
-        for h in range(2):
-            cols = slice(h * HALF, (h + 1) * HALF)
+
+        def group_rr(cols):
+            h, at = divmod(cols.start, HALF)
+            width = cols.stop - cols.start
+            rr = tile([P, width, PACK], BF16, "rr" + str(cols.start))
+            nc.vector.tensor_copy(
+                rr[:].rearrange("p (c i) t -> p c t i", i=4),
+                rr_rows[h][:, :, at : at + width].rearrange("p t (c i) -> p c t i", i=4),
+            )
+            return rr
+
+        def quantize_rr(cols, rr):
             nc.vector.quantize_mx(
                 out=rr_codes[:, cols].bitcast(FP8X4),
                 scales=rr_scales[:, cols],
-                in_=rr_halves[h][:].rearrange("p n t -> p (n t)"),
+                in_=rr[:].rearrange("p n t -> p (n t)"),
             )
 
         w2_grouped = tile([P, PACK, P, PACK], BF16, "w2_grouped")
-        deal_weights(nc.scalar.copy, w2_grouped, w2_raw[0], 0)
-        deal_weights(nc.scalar.copy, w2_grouped, w2_raw[1], 1)
-        w2_mx = quantize_weights(w2_grouped, "w2")
+        for h in range(2):
+            deal_weights(nc.scalar.copy, w2_grouped, w2_raw[h], h)
+
+        grouped = [group_rr(PIECES[0]), group_rr(PIECES[1])]
+        quantize_rr(PIECES[0], grouped[0])
+        grouped.append(group_rr(PIECES[2]))
+        quantize_rr(PIECES[1], grouped[1])
+        w2_mx = [quantize_weights(w2_grouped, "w2", 0)]
+        quantize_rr(PIECES[2], grouped[2])
+        w2_mx.extend(quantize_weights(w2_grouped, "w2", t) for t in range(1, PACK))
 
         f_rows = tile([P, PACK * S], F32, "f_rows")
-        for t in range(PACK):
-            width = HALF if t == 0 else S
-            for h in range(S // width):
-                cols = slice(h * width, (h + 1) * width)
-                bank = psum.tile([P, width], F32, name="bank%d%d" % (h, t))
-                product(bank, w2_mx[t], rr_codes[:, cols], rr_scales[:, cols])
-                nc.scalar.copy(out=f_rows[:, t * S + cols.start : t * S + cols.stop], in_=bank[:])
+        work = [(0, cols) for cols in PIECES] + [(t, slice(0, S)) for t in range(1, PACK)]
+        for i, (t, cols) in enumerate(work):
+            bank = psum.tile([P, cols.stop - cols.start], F32, name="bank" + str(i))
+            product(bank, w2_mx[t], rr_codes[:, cols], rr_scales[:, cols])
+            nc.scalar.copy(out=f_rows[:, t * S + cols.start : t * S + cols.stop], in_=bank[:])
 
         out_rows = out_0.rearrange("(p t) n -> p t n", t=PACK)
         out_words = out_1[0].rearrange("p n t -> p (n t)").bitcast(I32)

@@ -87,7 +87,7 @@ def tile_picked_ylbm_str_po_kernel(
                 stop=True,
             )
 
-        nc.vector.tensor_scalar(keep_sb[:], rate_sb[:], -1.0, 1.0, ALU.mult, ALU.add)
+        nc.scalar.activation(keep_sb[:], rate_sb[:], ACT.Copy, bias=1.0, scale=-1.0)
 
         x_scale = []
         for h in range(2):
@@ -96,10 +96,10 @@ def tile_picked_ylbm_str_po_kernel(
             x_scale.append(picked)
 
         w1_grouped = tile([P, PACK, P, PACK], BF16, "w1_grouped")
-        deal_weights(nc.scalar.copy, w1_grouped, w1_raw[0], 0)
+        deal_weights(nc.vector.tensor_copy, w1_grouped, w1_raw[0], 0)
         late = tile([P, 4 * PACK * HALF], F32, "late", "w1_raw0")
         parts = [late[:, i * PACK * HALF : (i + 1) * PACK * HALF] for i in range(4)]
-        eq_raw = [load_half(eq, 0, parts[0], 2), load_half(eq, 1, parts[1])]
+        eq_raw = [load_half(eq, 0, parts[0], 2), load_half(eq, 1, parts[1], 2)]
         w2_raw = [load_half(w2, h, parts[2 + h]) for h in range(2)]
         deal_weights(nc.vector.tensor_copy, w1_grouped, w1_raw[1], 1)
         w1_mx = [quantize_weights(w1_grouped, "w1", t) for t in range(PACK)]
@@ -178,17 +178,25 @@ def tile_picked_ylbm_str_po_kernel(
                 f_rows[:, t * S : window_end].indirect(src_sb[:, first // 16 : (first + width) // 16]),
             )
 
-        def hand_out(first, width, copy):
-            h, at = divmod(first, HALF)
-            cols = slice(first, first + width)
-            values = streamed[h][:, :, at : at + width]
-            nc.sync.dma_start(out=out_rows[:, :, cols], in_=values)
-            rounded = tile([P, width, PACK], BF16, "rounded" + str(first))
-            copy(
-                out=rounded[:].rearrange("p (c i) t -> p c t i", i=4),
-                in_=values.rearrange("p t (c i) -> p c t i", i=4),
+        def store(rows, cols):
+            h, at = divmod(cols.start, HALF)
+            nc.sync.dma_start(
+                out=out_rows[:, rows, cols], in_=streamed[h][:, rows, at : at + cols.stop - cols.start]
             )
-            codes = tile([P, width], I32, "out_codes" + str(first))
+
+        def hand_on(cols, copies):
+            h, at = divmod(cols.start, HALF)
+            width = cols.stop - cols.start
+            share = width // len(copies)
+            rounded = tile([P, width, PACK], BF16, "rounded" + str(cols.start))
+            for i, copy in enumerate(copies):
+                copy(
+                    out=rounded[:, i * share : (i + 1) * share, :].rearrange("p (c i) t -> p c t i", i=4),
+                    in_=streamed[h][:, :, at + i * share : at + (i + 1) * share].rearrange(
+                        "p t (c i) -> p c t i", i=4
+                    ),
+                )
+            codes = tile([P, width], I32, "out_codes" + str(cols.start))
             nc.vector.quantize_mx(
                 out=codes[:].bitcast(FP8X4),
                 scales=out_scales[:, cols],
@@ -198,15 +206,17 @@ def tile_picked_ylbm_str_po_kernel(
 
         for t in range(PACK):
             stream(t, 0, HALF, (t + 1) * S)
+        store(slice(0, PACK), PIECES[0])
         for t in range(2):
             stream(t, HALF, HALF, PACK * S)
-        for t in range(2, PACK):
-            stream(t, HALF, QUARTER, PACK * S)
-        hand_out(0, HALF, nc.scalar.copy)
-        for t in range(2, PACK):
-            stream(t, HALF + QUARTER, QUARTER, PACK * S)
-        hand_out(HALF, QUARTER, nc.scalar.copy)
-        hand_out(HALF + QUARTER, QUARTER, nc.vector.tensor_copy)
+        store(slice(0, 2), slice(HALF, S))
+        for first in (HALF, HALF + QUARTER):
+            for t in range(2, PACK):
+                stream(t, first, QUARTER, PACK * S)
+        store(slice(2, PACK), slice(HALF, S))
+        hand_on(PIECES[0], [nc.scalar.copy])
+        hand_on(PIECES[1], [nc.scalar.copy])
+        hand_on(PIECES[2], [nc.vector.tensor_copy, nc.scalar.copy])
         for q in range(4):
             queue = nc.sync if q % 2 else nc.scalar
             queue.dma_start(

@@ -19,6 +19,8 @@ P = 128
 PACK = 4
 HALF = 256
 QUARTER = 128
+W1_VECTOR = 352
+W2_VECTOR = 176
 PIECES = (slice(0, HALF), slice(HALF, HALF + QUARTER), slice(HALF + QUARTER, 2 * HALF))
 
 
@@ -48,22 +50,27 @@ def tile_picked_ylbm_str_po_kernel(
             return raw
 
         nc.vector.memset(xs_table[:].bitcast(I32), 0)
-        nc.sync.dma_start(offs_sb[:], offs)
         for q in range(4):
             nc.scalar.dma_start(
                 out=xs_table[32 * q : 32 * q + 4, :].bitcast(I32),
                 in_=x_scales[0, 4 * q : 4 * q + 4, :].bitcast(I32),
             )
         nc.scalar.dma_start(out=rate_sb[:], in_=rate.rearrange("(p t) o -> p (t o)", t=PACK))
-        w1_raw = [load_half(w1, h, tile([P, PACK * HALF], F32, "w1_raw" + str(h))[:]) for h in range(2)]
+        nc.sync.dma_start(offs_sb[:], offs)
+        w1_rows = w1.rearrange("(p j) c -> p j c", j=PACK)
+        w1_raw = [tile([P, 2, H], F32, "w1_raw" + str(u)) for u in range(2)]
+        for u in range(2):
+            nc.sync.dma_start(out=w1_raw[u][:], in_=w1_rows[:, 2 * u : 2 * u + 2, :])
+        nc.scalar.activation(keep_sb[:], rate_sb[:], ACT.Copy, bias=1.0, scale=-1.0)
         nc.sync.dma_start(out=xw_table[:], in_=x_words[0].rearrange("p n t -> p (n t)").bitcast(I32))
         nc.sync.dma_start(src_sb[:], src)
 
-        def deal_weights(copy, grouped, raw, h):
-            m = HALF // PACK
+        def deal_weights(copy, grouped, cols, raw, raw_first, rows=slice(0, PACK)):
             copy(
-                out=grouped[:, :, h * m : (h + 1) * m, :].rearrange("p t m j -> p m j t"),
-                in_=raw.rearrange("p j (m t) -> p m j t", t=PACK),
+                out=grouped[:, :, cols.start // PACK : cols.stop // PACK, rows].rearrange("p t m j -> p m j t"),
+                in_=raw[:, :, cols.start - raw_first : cols.stop - raw_first].rearrange(
+                    "p j (m t) -> p m j t", t=PACK
+                ),
             )
 
         def quantize_weights(grouped, name, t):
@@ -87,7 +94,6 @@ def tile_picked_ylbm_str_po_kernel(
                 stop=True,
             )
 
-        nc.scalar.activation(keep_sb[:], rate_sb[:], ACT.Copy, bias=1.0, scale=-1.0)
 
         x_scale = []
         for h in range(2):
@@ -96,12 +102,13 @@ def tile_picked_ylbm_str_po_kernel(
             x_scale.append(picked)
 
         w1_grouped = tile([P, PACK, P, PACK], BF16, "w1_grouped")
-        deal_weights(nc.vector.tensor_copy, w1_grouped, w1_raw[0], 0)
+        deal_weights(nc.vector.tensor_copy, w1_grouped, slice(0, H), w1_raw[0], 0, slice(0, 2))
+        deal_weights(nc.vector.tensor_copy, w1_grouped, slice(0, W1_VECTOR), w1_raw[1], 0, slice(2, PACK))
+        deal_weights(nc.scalar.copy, w1_grouped, slice(W1_VECTOR, H), w1_raw[1], 0, slice(2, PACK))
         late = tile([P, 4 * PACK * HALF], F32, "late", "w1_raw0")
         parts = [late[:, i * PACK * HALF : (i + 1) * PACK * HALF] for i in range(4)]
         eq_raw = [load_half(eq, 0, parts[0], 2), load_half(eq, 1, parts[1], 2)]
         w2_raw = [load_half(w2, h, parts[2 + h]) for h in range(2)]
-        deal_weights(nc.vector.tensor_copy, w1_grouped, w1_raw[1], 1)
         w1_mx = [quantize_weights(w1_grouped, "w1", t) for t in range(PACK)]
 
         x_word = []
@@ -148,16 +155,16 @@ def tile_picked_ylbm_str_po_kernel(
             )
 
         w2_grouped = tile([P, PACK, P, PACK], BF16, "w2_grouped")
-        for h in range(2):
-            deal_weights(nc.scalar.copy, w2_grouped, w2_raw[h], h)
+        deal_weights(nc.scalar.copy, w2_grouped, slice(0, HALF), w2_raw[0], 0)
+        deal_weights(nc.scalar.copy, w2_grouped, slice(HALF, N - W2_VECTOR), w2_raw[1], HALF)
 
         grouped = [group_rr(PIECES[0]), group_rr(PIECES[1])]
         quantize_rr(PIECES[0], grouped[0])
         grouped.append(group_rr(PIECES[2]))
         quantize_rr(PIECES[1], grouped[1])
-        w2_mx = [quantize_weights(w2_grouped, "w2", 0)]
         quantize_rr(PIECES[2], grouped[2])
-        w2_mx.extend(quantize_weights(w2_grouped, "w2", t) for t in range(1, PACK))
+        deal_weights(nc.vector.tensor_copy, w2_grouped, slice(N - W2_VECTOR, N), w2_raw[1], HALF)
+        w2_mx = [quantize_weights(w2_grouped, "w2", t) for t in range(PACK)]
 
         f_rows = tile([P, PACK * S], F32, "f_rows")
         work = [(0, cols) for cols in PIECES] + [(t, slice(0, S)) for t in range(1, PACK)]

@@ -20,7 +20,8 @@ PACK = 4
 HALF = 256
 QUARTER = 128
 W1_VECTOR = 352
-W2_VECTOR = 176
+RR_SCALAR = 192
+W2_SCALAR = 192
 PIECES = (slice(0, HALF), slice(HALF, HALF + QUARTER), slice(HALF + QUARTER, 2 * HALF))
 
 
@@ -41,13 +42,9 @@ def tile_picked_ylbm_str_po_kernel(
         xw_table = tile([P, T], I32, "xw_table")
         rate_sb = tile([P, PACK], F32, "rate_sb")
         keep_sb = tile([P, PACK], F32, "keep_sb")
-
-        def load_half(dram, h, raw, step=PACK):
-            rows = dram.rearrange("(p j) c -> p j c", j=PACK)
-            raw = raw.rearrange("p (j c) -> p j c", j=PACK)
-            for j in range(0, PACK, step):
-                nc.sync.dma_start(out=raw[:, j : j + step, :], in_=rows[:, j : j + step, h * HALF : (h + 1) * HALF])
-            return raw
+        w1_raw = tile([P, PACK, H], F32, "w1_raw")
+        w2_raw = tile([P, PACK, N], F32, "w2_raw")
+        eq_raw = [tile([P, S], F32, "eq_raw" + str(t)) for t in range(PACK)]
 
         nc.vector.memset(xs_table[:].bitcast(I32), 0)
         for q in range(4):
@@ -57,20 +54,19 @@ def tile_picked_ylbm_str_po_kernel(
             )
         nc.scalar.dma_start(out=rate_sb[:], in_=rate.rearrange("(p t) o -> p (t o)", t=PACK))
         nc.sync.dma_start(offs_sb[:], offs)
-        w1_rows = w1.rearrange("(p j) c -> p j c", j=PACK)
-        w1_raw = [tile([P, 2, H], F32, "w1_raw" + str(u)) for u in range(2)]
-        for u in range(2):
-            nc.sync.dma_start(out=w1_raw[u][:], in_=w1_rows[:, 2 * u : 2 * u + 2, :])
-        nc.scalar.activation(keep_sb[:], rate_sb[:], ACT.Copy, bias=1.0, scale=-1.0)
-        nc.sync.dma_start(out=xw_table[:], in_=x_words[0].rearrange("p n t -> p (n t)").bitcast(I32))
+        nc.sync.dma_start(out=w1_raw[:], in_=w1.rearrange("(p j) c -> p j c", j=PACK))
         nc.sync.dma_start(src_sb[:], src)
+        nc.sync.dma_start(out=xw_table[:], in_=x_words[0].rearrange("p n t -> p (n t)").bitcast(I32))
+        eq_rows = eq.rearrange("(p t) c -> p t c", t=PACK)
+        for t in range(PACK):
+            nc.sync.dma_start(out=eq_raw[t][:], in_=eq_rows[:, t, :])
+        nc.sync.dma_start(out=w2_raw[:], in_=w2.rearrange("(p j) c -> p j c", j=PACK))
+        nc.scalar.activation(keep_sb[:], rate_sb[:], ACT.Copy, bias=1.0, scale=-1.0)
 
-        def deal_weights(copy, grouped, cols, raw, raw_first, rows=slice(0, PACK)):
+        def deal_weights(copy, grouped, raw, cols, sets=slice(0, PACK)):
             copy(
-                out=grouped[:, :, cols.start // PACK : cols.stop // PACK, rows].rearrange("p t m j -> p m j t"),
-                in_=raw[:, :, cols.start - raw_first : cols.stop - raw_first].rearrange(
-                    "p j (m t) -> p m j t", t=PACK
-                ),
+                out=grouped[:, sets, cols.start // PACK : cols.stop // PACK, :].rearrange("p t m j -> p m j t"),
+                in_=raw[:, :, cols].rearrange("p j (m t) -> p m j t", t=PACK)[:, :, :, sets],
             )
 
         def quantize_weights(grouped, name, t):
@@ -94,21 +90,12 @@ def tile_picked_ylbm_str_po_kernel(
                 stop=True,
             )
 
-
-        x_scale = []
-        for h in range(2):
-            picked = tile([P, HALF], U8, "x_scale" + str(h))
-            nc.vector.tensor_copy(picked[:], xs_table[:].indirect(offs_sb[:, 16 * h : 16 * (h + 1)]))
-            x_scale.append(picked)
+        x_scale = tile([P, S], U8, "x_scale")
+        nc.vector.tensor_copy(x_scale[:], xs_table[:].indirect(offs_sb[:]))
 
         w1_grouped = tile([P, PACK, P, PACK], BF16, "w1_grouped")
-        deal_weights(nc.vector.tensor_copy, w1_grouped, slice(0, H), w1_raw[0], 0, slice(0, 2))
-        deal_weights(nc.vector.tensor_copy, w1_grouped, slice(0, W1_VECTOR), w1_raw[1], 0, slice(2, PACK))
-        deal_weights(nc.scalar.copy, w1_grouped, slice(W1_VECTOR, H), w1_raw[1], 0, slice(2, PACK))
-        late = tile([P, 4 * PACK * HALF], F32, "late", "w1_raw0")
-        parts = [late[:, i * PACK * HALF : (i + 1) * PACK * HALF] for i in range(4)]
-        eq_raw = [load_half(eq, 0, parts[0], 2), load_half(eq, 1, parts[1], 2)]
-        w2_raw = [load_half(w2, h, parts[2 + h]) for h in range(2)]
+        deal_weights(nc.vector.tensor_copy, w1_grouped, w1_raw, slice(0, W1_VECTOR))
+        deal_weights(nc.scalar.copy, w1_grouped, w1_raw, slice(W1_VECTOR, H))
         w1_mx = [quantize_weights(w1_grouped, "w1", t) for t in range(PACK)]
 
         x_word = []
@@ -120,54 +107,52 @@ def tile_picked_ylbm_str_po_kernel(
             )
             x_word.append(picked)
 
-
-        rr_rows = []
-        for h in range(2):
-            pull = tile([P, PACK, HALF], F32, "pull" + str(h))
-            rows = tile([P, PACK, HALF], BF16, "rr_rows" + str(h))
-            for t in range(PACK):
-                nc.scalar.activation(pull[:, t, :], eq_raw[h][:, t, :], ACT.Copy, scale=rate_sb[:, t : t + 1])
-                bank = psum.tile([P, HALF], F32, name="bank" + str(PACK * h + t))
-                product(bank, w1_mx[t], x_word[h][:], x_scale[h][:])
+        rr_rows = [tile([P, PACK, HALF], BF16, "rr_rows" + str(h)) for h in range(2)]
+        for t in range(PACK):
+            pull = tile([P, S], F32, "pull" + str(t))
+            nc.scalar.activation(pull[:], eq_raw[t][:], ACT.Copy, scale=rate_sb[:, t : t + 1])
+            for h in range(2):
+                cols = slice(h * HALF, (h + 1) * HALF)
+                bank = psum.tile([P, HALF], F32, name="bank" + str(2 * t + h))
+                product(bank, w1_mx[t], x_word[h][:], x_scale[:, cols])
                 nc.vector.scalar_tensor_tensor(
-                    rows[:, t, :], bank[:], keep_sb[:, t : t + 1], pull[:, t, :], ALU.mult, ALU.add
+                    rr_rows[h][:, t, :], bank[:], keep_sb[:, t : t + 1], pull[:, cols], ALU.mult, ALU.add
                 )
-            rr_rows.append(rows)
 
         rr_codes = tile([P, S], I32, "rr_codes")
         rr_scales = tile([P, S], U8, "rr_scales")
+        rr = [tile([P, HALF, PACK], BF16, "rr" + str(h)) for h in range(2)]
 
-        def group_rr(cols):
-            h, at = divmod(cols.start, HALF)
-            width = cols.stop - cols.start
-            rr = tile([P, width, PACK], BF16, "rr" + str(cols.start))
-            nc.vector.tensor_copy(
-                rr[:].rearrange("p (c i) t -> p c t i", i=4),
-                rr_rows[h][:, :, at : at + width].rearrange("p t (c i) -> p c t i", i=4),
+        def group_rr(copy, h, cols):
+            copy(
+                out=rr[h][:, cols, :].rearrange("p (c i) t -> p c t i", i=4),
+                in_=rr_rows[h][:, :, cols].rearrange("p t (c i) -> p c t i", i=4),
             )
-            return rr
 
-        def quantize_rr(cols, rr):
+        def quantize_rr(h):
+            cols = slice(h * HALF, (h + 1) * HALF)
             nc.vector.quantize_mx(
                 out=rr_codes[:, cols].bitcast(FP8X4),
                 scales=rr_scales[:, cols],
-                in_=rr[:].rearrange("p n t -> p (n t)"),
+                in_=rr[h][:].rearrange("p n t -> p (n t)"),
             )
 
-        w2_grouped = tile([P, PACK, P, PACK], BF16, "w2_grouped")
-        deal_weights(nc.scalar.copy, w2_grouped, slice(0, HALF), w2_raw[0], 0)
-        deal_weights(nc.scalar.copy, w2_grouped, slice(HALF, N - W2_VECTOR), w2_raw[1], HALF)
+        group_rr(nc.scalar.copy, 0, slice(0, RR_SCALAR))
+        group_rr(nc.vector.tensor_copy, 1, slice(0, HALF))
+        group_rr(nc.vector.tensor_copy, 0, slice(RR_SCALAR, HALF))
+        quantize_rr(1)
+        quantize_rr(0)
 
-        grouped = [group_rr(PIECES[0]), group_rr(PIECES[1])]
-        quantize_rr(PIECES[0], grouped[0])
-        grouped.append(group_rr(PIECES[2]))
-        quantize_rr(PIECES[1], grouped[1])
-        quantize_rr(PIECES[2], grouped[2])
-        deal_weights(nc.vector.tensor_copy, w2_grouped, slice(N - W2_VECTOR, N), w2_raw[1], HALF)
+        w2_grouped = tile([P, PACK, P, PACK], BF16, "w2_grouped")
+        w2_mx = []
+        for u in range(2):
+            sets = slice(2 * u, 2 * u + 2)
+            deal_weights(nc.scalar.copy, w2_grouped, w2_raw, slice(0, W2_SCALAR), sets)
+            deal_weights(nc.vector.tensor_copy, w2_grouped, w2_raw, slice(W2_SCALAR, N), sets)
         w2_mx = [quantize_weights(w2_grouped, "w2", t) for t in range(PACK)]
 
         f_rows = tile([P, PACK * S], F32, "f_rows")
-        work = [(0, cols) for cols in PIECES] + [(t, slice(0, S)) for t in range(1, PACK)]
+        work = [(0, slice(0, HALF)), (0, slice(HALF, S))] + [(t, slice(0, S)) for t in range(1, PACK)]
         for i, (t, cols) in enumerate(work):
             bank = psum.tile([P, cols.stop - cols.start], F32, name="bank" + str(i))
             product(bank, w2_mx[t], rr_codes[:, cols], rr_scales[:, cols])

@@ -20,8 +20,7 @@ PACK = 4
 HALF = 256
 QUARTER = 128
 W1_VECTOR = 352
-RR_SCALAR = 192
-W2_SCALAR = 192
+W2_VECTOR = 128
 PIECES = (slice(0, HALF), slice(HALF, HALF + QUARTER), slice(HALF + QUARTER, 2 * HALF))
 
 
@@ -43,30 +42,38 @@ def tile_picked_ylbm_str_po_kernel(
         rate_sb = tile([P, PACK], F32, "rate_sb")
         keep_sb = tile([P, PACK], F32, "keep_sb")
         w1_raw = tile([P, PACK, H], F32, "w1_raw")
-        w2_raw = tile([P, PACK, N], F32, "w2_raw")
-        eq_raw = [tile([P, S], F32, "eq_raw" + str(t)) for t in range(PACK)]
+        w2_raw = [tile([P, PACK, HALF], F32, "w2_raw" + str(h)) for h in range(2)]
+        eq_raw = tile([P, PACK, S], F32, "eq_raw")
 
-        nc.vector.memset(xs_table[:].bitcast(I32), 0)
+        nc.vector.memset(xs_table[:, : T // 2].bitcast(I32), 0)
+        nc.gpsimd.memset(xs_table[:, T // 2 :].bitcast(I32), 0)
+        nc.sync.dma_start(offs_sb[:], offs)
+        w1_rows = w1.rearrange("(p j) c -> p j c", j=PACK)
+        nc.sync.dma_start(out=w1_raw[:, 0:1, :], in_=w1_rows[:, 0:1, :])
         for q in range(4):
-            nc.scalar.dma_start(
+            queue = nc.sync if q % 2 else nc.scalar
+            queue.dma_start(
                 out=xs_table[32 * q : 32 * q + 4, :].bitcast(I32),
                 in_=x_scales[0, 4 * q : 4 * q + 4, :].bitcast(I32),
             )
+        nc.sync.dma_start(out=w1_raw[:, 1:PACK, :], in_=w1_rows[:, 1:PACK, :])
         nc.scalar.dma_start(out=rate_sb[:], in_=rate.rearrange("(p t) o -> p (t o)", t=PACK))
-        nc.sync.dma_start(offs_sb[:], offs)
-        nc.sync.dma_start(out=w1_raw[:], in_=w1.rearrange("(p j) c -> p j c", j=PACK))
-        nc.sync.dma_start(src_sb[:], src)
         nc.sync.dma_start(out=xw_table[:], in_=x_words[0].rearrange("p n t -> p (n t)").bitcast(I32))
         eq_rows = eq.rearrange("(p t) c -> p t c", t=PACK)
-        for t in range(PACK):
-            nc.sync.dma_start(out=eq_raw[t][:], in_=eq_rows[:, t, :])
-        nc.sync.dma_start(out=w2_raw[:], in_=w2.rearrange("(p j) c -> p j c", j=PACK))
+        for sets in (slice(0, 2), slice(2, 3), slice(3, PACK)):
+            nc.sync.dma_start(out=eq_raw[:, sets, :], in_=eq_rows[:, sets, :])
+        w2_rows = w2.rearrange("(p j) c -> p j c", j=PACK)
+        for h in range(2):
+            nc.sync.dma_start(out=w2_raw[h][:], in_=w2_rows[:, :, h * HALF : (h + 1) * HALF])
+        nc.sync.dma_start(src_sb[:], src)
         nc.scalar.activation(keep_sb[:], rate_sb[:], ACT.Copy, bias=1.0, scale=-1.0)
 
-        def deal_weights(copy, grouped, raw, cols, sets=slice(0, PACK)):
+        def deal_weights(copy, grouped, raw, cols, raw_first=0, sets=slice(0, PACK)):
             copy(
                 out=grouped[:, sets, cols.start // PACK : cols.stop // PACK, :].rearrange("p t m j -> p m j t"),
-                in_=raw[:, :, cols].rearrange("p j (m t) -> p m j t", t=PACK)[:, :, :, sets],
+                in_=raw[:, :, cols.start - raw_first : cols.stop - raw_first].rearrange(
+                    "p j (m t) -> p m j t", t=PACK
+                )[:, :, :, sets],
             )
 
         def quantize_weights(grouped, name, t):
@@ -107,59 +114,68 @@ def tile_picked_ylbm_str_po_kernel(
             )
             x_word.append(picked)
 
-        rr_rows = [tile([P, PACK, HALF], BF16, "rr_rows" + str(h)) for h in range(2)]
-        for t in range(PACK):
-            pull = tile([P, S], F32, "pull" + str(t))
-            nc.scalar.activation(pull[:], eq_raw[t][:], ACT.Copy, scale=rate_sb[:, t : t + 1])
-            for h in range(2):
-                cols = slice(h * HALF, (h + 1) * HALF)
-                bank = psum.tile([P, HALF], F32, name="bank" + str(2 * t + h))
+        halves = [slice(h * HALF, (h + 1) * HALF) for h in range(2)]
+        pull = tile([P, PACK, S], F32, "pull")
+
+        def make_pull(t, cols):
+            nc.vector.tensor_scalar(pull[:, t, cols], eq_raw[:, t, cols], rate_sb[:, t : t + 1], None, ALU.mult)
+
+        for t in range(PACK - 1):
+            make_pull(t, slice(0, S))
+
+        rr = []
+        for h, cols in enumerate(halves):
+            kept = tile([P, PACK, HALF], F32, "kept" + str(h))
+            for t in range(PACK):
+                bank = psum.tile([P, HALF], F32, name="bank" + str(PACK * h + t))
                 product(bank, w1_mx[t], x_word[h][:], x_scale[:, cols])
-                nc.vector.scalar_tensor_tensor(
-                    rr_rows[h][:, t, :], bank[:], keep_sb[:, t : t + 1], pull[:, cols], ALU.mult, ALU.add
-                )
+                nc.scalar.activation(kept[:, t, :], bank[:], ACT.Copy, scale=keep_sb[:, t : t + 1])
+            make_pull(PACK - 1, cols)
+            relaxed = tile([P, HALF, PACK], BF16, "rr" + str(h))
+            nc.vector.tensor_tensor(
+                relaxed[:].rearrange("p (c i) t -> p c t i", i=4),
+                kept[:].rearrange("p t (c i) -> p c t i", i=4),
+                pull[:, :, cols].rearrange("p t (c i) -> p c t i", i=4),
+                ALU.add,
+            )
+            rr.append(relaxed)
 
         rr_codes = tile([P, S], I32, "rr_codes")
         rr_scales = tile([P, S], U8, "rr_scales")
-        rr = [tile([P, HALF, PACK], BF16, "rr" + str(h)) for h in range(2)]
-
-        def group_rr(copy, h, cols):
-            copy(
-                out=rr[h][:, cols, :].rearrange("p (c i) t -> p c t i", i=4),
-                in_=rr_rows[h][:, :, cols].rearrange("p t (c i) -> p c t i", i=4),
-            )
 
         def quantize_rr(h):
-            cols = slice(h * HALF, (h + 1) * HALF)
             nc.vector.quantize_mx(
-                out=rr_codes[:, cols].bitcast(FP8X4),
-                scales=rr_scales[:, cols],
+                out=rr_codes[:, halves[h]].bitcast(FP8X4),
+                scales=rr_scales[:, halves[h]],
                 in_=rr[h][:].rearrange("p n t -> p (n t)"),
             )
 
-        group_rr(nc.scalar.copy, 0, slice(0, RR_SCALAR))
-        group_rr(nc.vector.tensor_copy, 1, slice(0, HALF))
-        group_rr(nc.vector.tensor_copy, 0, slice(RR_SCALAR, HALF))
-        quantize_rr(1)
+        w2_grouped = tile([P, PACK, P, PACK], BF16, "w2_grouped", "w1_codes3")
+        first, second = slice(0, 2), slice(2, PACK)
+        deal_weights(nc.scalar.copy, w2_grouped, w2_raw[0], halves[0])
+        deal_weights(nc.scalar.copy, w2_grouped, w2_raw[1], slice(HALF, N - W2_VECTOR), HALF, first)
         quantize_rr(0)
-
-        w2_grouped = tile([P, PACK, P, PACK], BF16, "w2_grouped")
-        w2_mx = []
-        for u in range(2):
-            sets = slice(2 * u, 2 * u + 2)
-            deal_weights(nc.scalar.copy, w2_grouped, w2_raw, slice(0, W2_SCALAR), sets)
-            deal_weights(nc.vector.tensor_copy, w2_grouped, w2_raw, slice(W2_SCALAR, N), sets)
-        w2_mx = [quantize_weights(w2_grouped, "w2", t) for t in range(PACK)]
+        deal_weights(nc.vector.tensor_copy, w2_grouped, w2_raw[1], slice(N - W2_VECTOR, N), HALF, first)
+        quantize_rr(1)
+        w2_mx = [quantize_weights(w2_grouped, "w2", t) for t in range(2)]
+        deal_weights(nc.vector.tensor_copy, w2_grouped, w2_raw[1], halves[1], HALF, second)
+        w2_mx.extend(quantize_weights(w2_grouped, "w2", t) for t in range(2, PACK))
 
         f_rows = tile([P, PACK * S], F32, "f_rows")
-        work = [(0, slice(0, HALF)), (0, slice(HALF, S))] + [(t, slice(0, S)) for t in range(1, PACK)]
-        for i, (t, cols) in enumerate(work):
+
+        def populations(i, t, cols, copy):
             bank = psum.tile([P, cols.stop - cols.start], F32, name="bank" + str(i))
             product(bank, w2_mx[t], rr_codes[:, cols], rr_scales[:, cols])
-            nc.scalar.copy(out=f_rows[:, t * S + cols.start : t * S + cols.stop], in_=bank[:])
+            copy(out=f_rows[:, t * S + cols.start : t * S + cols.stop], in_=bank[:])
+
+        populations(0, 0, halves[0], nc.scalar.copy)
+        populations(1, 0, halves[1], nc.scalar.copy)
+        for t in range(1, PACK):
+            populations(1 + t, t, slice(0, S), nc.scalar.copy)
 
         out_rows = out_0.rearrange("(p t) n -> p t n", t=PACK)
         out_words = out_1[0].rearrange("p n t -> p (n t)").bitcast(I32)
+        out_codes = tile([P, S], I32, "out_codes")
         out_scales = tile([P, S], U8, "out_scales")
         streamed = [tile([P, PACK, HALF], F32, "streamed" + str(h)) for h in range(2)]
 
@@ -188,27 +204,28 @@ def tile_picked_ylbm_str_po_kernel(
                         "p t (c i) -> p c t i", i=4
                     ),
                 )
-            codes = tile([P, width], I32, "out_codes" + str(cols.start))
             nc.vector.quantize_mx(
-                out=codes[:].bitcast(FP8X4),
+                out=out_codes[:, cols].bitcast(FP8X4),
                 scales=out_scales[:, cols],
                 in_=rounded[:].rearrange("p n t -> p (n t)"),
             )
-            nc.sync.dma_start(out=out_words[:, cols], in_=codes[:])
 
         for t in range(PACK):
             stream(t, 0, HALF, (t + 1) * S)
-        store(slice(0, PACK), PIECES[0])
+            if t % 2:
+                store(slice(t - 1, t + 1), PIECES[0])
         for t in range(2):
             stream(t, HALF, HALF, PACK * S)
         store(slice(0, 2), slice(HALF, S))
         for first in (HALF, HALF + QUARTER):
             for t in range(2, PACK):
                 stream(t, first, QUARTER, PACK * S)
-        store(slice(2, PACK), slice(HALF, S))
+            store(slice(2, PACK), slice(first, first + QUARTER))
         hand_on(PIECES[0], [nc.scalar.copy])
+        nc.sync.dma_start(out=out_words[:, halves[0]], in_=out_codes[:, halves[0]])
         hand_on(PIECES[1], [nc.scalar.copy])
         hand_on(PIECES[2], [nc.vector.tensor_copy, nc.scalar.copy])
+        nc.sync.dma_start(out=out_words[:, halves[1]], in_=out_codes[:, halves[1]])
         for q in range(4):
             queue = nc.sync if q % 2 else nc.scalar
             queue.dma_start(

@@ -21,6 +21,7 @@ HALF = 256
 QUARTER = 128
 W1_VECTOR = 352
 W2_VECTOR = 128
+WIDE = 704
 PIECES = (slice(0, HALF), slice(HALF, HALF + QUARTER), slice(HALF + QUARTER, 2 * HALF))
 
 
@@ -163,68 +164,66 @@ def tile_picked_ylbm_str_po_kernel(
 
         f_rows = tile([P, PACK * S], F32, "f_rows")
 
-        def populations(i, t, cols, copy):
+        def f_start(t):
+            return (PACK - 1 - t) * S
+
+        def populations(i, t, cols):
             bank = psum.tile([P, cols.stop - cols.start], F32, name="bank" + str(i))
             product(bank, w2_mx[t], rr_codes[:, cols], rr_scales[:, cols])
-            copy(out=f_rows[:, t * S + cols.start : t * S + cols.stop], in_=bank[:])
+            nc.scalar.copy(out=f_rows[:, f_start(t) + cols.start : f_start(t) + cols.stop], in_=bank[:])
 
-        populations(0, 0, halves[0], nc.scalar.copy)
-        populations(1, 0, halves[1], nc.scalar.copy)
+        populations(0, 0, halves[0])
+        populations(1, 0, halves[1])
         for t in range(1, PACK):
-            populations(1 + t, t, slice(0, S), nc.scalar.copy)
+            populations(1 + t, t, slice(0, S))
 
         out_rows = out_0.rearrange("(p t) n -> p t n", t=PACK)
         out_words = out_1[0].rearrange("p n t -> p (n t)").bitcast(I32)
         out_codes = tile([P, S], I32, "out_codes")
         out_scales = tile([P, S], U8, "out_scales")
-        streamed = [tile([P, PACK, HALF], F32, "streamed" + str(h)) for h in range(2)]
+        streamed = tile([P, PACK, S], F32, "streamed")
+        rounded = tile([P, S, PACK], BF16, "rounded")
 
-        def stream(t, first, width, window_end):
-            h, at = divmod(first, HALF)
+        def stream(t, cols, window=S):
             nc.vector.tensor_copy(
-                streamed[h][:, t, at : at + width],
-                f_rows[:, t * S : window_end].indirect(src_sb[:, first // 16 : (first + width) // 16]),
+                streamed[:, t, cols],
+                f_rows[:, f_start(t) : f_start(t) + window].indirect(src_sb[:, cols.start // 16 : cols.stop // 16]),
             )
 
         def store(rows, cols):
-            h, at = divmod(cols.start, HALF)
-            nc.sync.dma_start(
-                out=out_rows[:, rows, cols], in_=streamed[h][:, rows, at : at + cols.stop - cols.start]
+            nc.sync.dma_start(out=out_rows[:, rows, cols], in_=streamed[:, rows, cols])
+
+        def round_pair(copy, rows, cols):
+            copy(
+                out=rounded[:, cols, rows].rearrange("p (c i) t -> p c t i", i=4),
+                in_=streamed[:, rows, cols].rearrange("p t (c i) -> p c t i", i=4),
             )
 
-        def hand_on(cols, copies):
-            h, at = divmod(cols.start, HALF)
-            width = cols.stop - cols.start
-            share = width // len(copies)
-            rounded = tile([P, width, PACK], BF16, "rounded" + str(cols.start))
-            for i, copy in enumerate(copies):
-                copy(
-                    out=rounded[:, i * share : (i + 1) * share, :].rearrange("p (c i) t -> p c t i", i=4),
-                    in_=streamed[h][:, :, at + i * share : at + (i + 1) * share].rearrange(
-                        "p t (c i) -> p c t i", i=4
-                    ),
-                )
+        def quantize_out(cols):
             nc.vector.quantize_mx(
                 out=out_codes[:, cols].bitcast(FP8X4),
                 scales=out_scales[:, cols],
-                in_=rounded[:].rearrange("p n t -> p (n t)"),
+                in_=rounded[:, cols, :].rearrange("p n t -> p (n t)"),
             )
 
-        for t in range(PACK):
-            stream(t, 0, HALF, (t + 1) * S)
-            if t % 2:
-                store(slice(t - 1, t + 1), PIECES[0])
-        for t in range(2):
-            stream(t, HALF, HALF, PACK * S)
-        store(slice(0, 2), slice(HALF, S))
-        for first in (HALF, HALF + QUARTER):
-            for t in range(2, PACK):
-                stream(t, first, QUARTER, PACK * S)
-            store(slice(2, PACK), slice(first, first + QUARTER))
-        hand_on(PIECES[0], [nc.scalar.copy])
+        whole = slice(0, S)
+        for cols in halves:
+            stream(0, cols)
+        stream(1, whole, WIDE)
+        store(first, whole)
+        round_pair(nc.scalar.copy, first, whole)
+        stream(2, whole, WIDE)
+        store(slice(2, 3), whole)
+        for cols in PIECES:
+            stream(3, cols)
+        store(slice(3, PACK), whole)
+        round_pair(nc.scalar.copy, second, PIECES[0])
+        round_pair(nc.scalar.copy, second, PIECES[1])
+        quantize_out(PIECES[0])
         nc.sync.dma_start(out=out_words[:, halves[0]], in_=out_codes[:, halves[0]])
-        hand_on(PIECES[1], [nc.scalar.copy])
-        hand_on(PIECES[2], [nc.vector.tensor_copy, nc.scalar.copy])
+        round_pair(nc.vector.tensor_copy, second, PIECES[2])
+        quantize_out(PIECES[1])
+        quantize_out(PIECES[2])
         nc.sync.dma_start(out=out_words[:, halves[1]], in_=out_codes[:, halves[1]])
         for q in range(4):
             queue = nc.sync if q % 2 else nc.scalar

@@ -19,7 +19,7 @@ P = 128
 PACK = 4
 HALF = 256
 QUARTER = 128
-W1_VECTOR = 352
+W1_VECTOR = (192, 352)
 W2_VECTOR = 128
 WIDE = 704
 PIECES = (slice(0, HALF), slice(HALF, HALF + QUARTER), slice(HALF + QUARTER, 2 * HALF))
@@ -43,38 +43,26 @@ def tile_picked_ylbm_str_po_kernel(
         rate_sb = tile([P, PACK], F32, "rate_sb")
         keep_sb = tile([P, PACK], F32, "keep_sb")
         w1_raw = tile([P, PACK, H], F32, "w1_raw")
-        w2_raw = [tile([P, PACK, HALF], F32, "w2_raw" + str(h)) for h in range(2)]
-        eq_raw = tile([P, PACK, S], F32, "eq_raw")
+        x_scale = tile([P, S], U8, "x_scale")
 
+        first, second = slice(0, 2), slice(2, PACK)
         nc.vector.memset(xs_table[:, : T // 2].bitcast(I32), 0)
         nc.gpsimd.memset(xs_table[:, T // 2 :].bitcast(I32), 0)
-        nc.sync.dma_start(offs_sb[:], offs)
+        nc.gpsimd.memset(x_scale[:].bitcast(I32), 0)
         w1_rows = w1.rearrange("(p j) c -> p j c", j=PACK)
         nc.sync.dma_start(out=w1_raw[:, 0:1, :], in_=w1_rows[:, 0:1, :])
-        for q in range(4):
-            queue = nc.sync if q % 2 else nc.scalar
-            queue.dma_start(
-                out=xs_table[32 * q : 32 * q + 4, :].bitcast(I32),
-                in_=x_scales[0, 4 * q : 4 * q + 4, :].bitcast(I32),
-            )
-        nc.sync.dma_start(out=w1_raw[:, 1:PACK, :], in_=w1_rows[:, 1:PACK, :])
+        nc.sync.dma_start(offs_sb[:], offs)
+        nc.sync.dma_start(out=xs_table[0:P:8, :].bitcast(I32), in_=x_scales[0].bitcast(I32))
+        nc.sync.dma_start(out=w1_raw[:, 1:2, :], in_=w1_rows[:, 1:2, :])
+        nc.sync.dma_start(out=w1_raw[:, second, :], in_=w1_rows[:, second, :])
         nc.scalar.dma_start(out=rate_sb[:], in_=rate.rearrange("(p t) o -> p (t o)", t=PACK))
         nc.sync.dma_start(out=xw_table[:], in_=x_words[0].rearrange("p n t -> p (n t)").bitcast(I32))
-        eq_rows = eq.rearrange("(p t) c -> p t c", t=PACK)
-        for sets in (slice(0, 2), slice(2, 3), slice(3, PACK)):
-            nc.sync.dma_start(out=eq_raw[:, sets, :], in_=eq_rows[:, sets, :])
-        w2_rows = w2.rearrange("(p j) c -> p j c", j=PACK)
-        for h in range(2):
-            nc.sync.dma_start(out=w2_raw[h][:], in_=w2_rows[:, :, h * HALF : (h + 1) * HALF])
-        nc.sync.dma_start(src_sb[:], src)
         nc.scalar.activation(keep_sb[:], rate_sb[:], ACT.Copy, bias=1.0, scale=-1.0)
 
-        def deal_weights(copy, grouped, raw, cols, raw_first=0, sets=slice(0, PACK)):
+        def deal_weights(copy, grouped, raw, cols, sets=slice(0, PACK), rows=slice(0, PACK)):
             copy(
-                out=grouped[:, sets, cols.start // PACK : cols.stop // PACK, :].rearrange("p t m j -> p m j t"),
-                in_=raw[:, :, cols.start - raw_first : cols.stop - raw_first].rearrange(
-                    "p j (m t) -> p m j t", t=PACK
-                )[:, :, :, sets],
+                out=grouped[:, sets, cols.start // PACK : cols.stop // PACK, rows].rearrange("p t m j -> p m j t"),
+                in_=raw[:, rows, cols].rearrange("p j (m t) -> p m j t", t=PACK)[:, :, :, sets],
             )
 
         def quantize_weights(grouped, name, t):
@@ -98,12 +86,28 @@ def tile_picked_ylbm_str_po_kernel(
                 stop=True,
             )
 
-        x_scale = tile([P, S], U8, "x_scale")
-        nc.vector.tensor_copy(x_scale[:], xs_table[:].indirect(offs_sb[:]))
+        xs_picked = tile([P, S], U8, "xs_picked")
+        nc.vector.tensor_copy(xs_picked[:], xs_table[:].indirect(offs_sb[:]))
+        for q in range(4):
+            nc.sync.dma_start(
+                out=x_scale[32 * q : 32 * q + 4, :].bitcast(I32),
+                in_=xs_picked[32 * q : 32 * (q + 1) : 8, :].bitcast(I32),
+            )
+        late = tile([P, 2 * PACK * S], F32, "late", "xs_table")
+        eq_raw = late[:, : PACK * S].rearrange("p (t c) -> p t c", t=PACK)
+        w2_raw = late[:, PACK * S :].rearrange("p (j c) -> p j c", j=PACK)
+        eq_rows = eq.rearrange("(p t) c -> p t c", t=PACK)
+        for sets in (slice(0, 2), slice(2, 3), slice(3, PACK)):
+            nc.sync.dma_start(out=eq_raw[:, sets, :], in_=eq_rows[:, sets, :])
+        w2_rows = w2.rearrange("(p j) c -> p j c", j=PACK)
+        for pair in (first, second):
+            nc.sync.dma_start(out=w2_raw[:, pair, :], in_=w2_rows[:, pair, :])
+        nc.sync.dma_start(src_sb[:], src)
 
         w1_grouped = tile([P, PACK, P, PACK], BF16, "w1_grouped")
-        deal_weights(nc.vector.tensor_copy, w1_grouped, w1_raw, slice(0, W1_VECTOR))
-        deal_weights(nc.scalar.copy, w1_grouped, w1_raw, slice(W1_VECTOR, H))
+        for pair, share in zip((first, second), W1_VECTOR):
+            deal_weights(nc.vector.tensor_copy, w1_grouped, w1_raw, slice(0, share), rows=pair)
+            deal_weights(nc.scalar.copy, w1_grouped, w1_raw, slice(share, H), rows=pair)
         w1_mx = [quantize_weights(w1_grouped, "w1", t) for t in range(PACK)]
 
         x_word = []
@@ -152,14 +156,14 @@ def tile_picked_ylbm_str_po_kernel(
             )
 
         w2_grouped = tile([P, PACK, P, PACK], BF16, "w2_grouped", "w1_codes3")
-        first, second = slice(0, 2), slice(2, PACK)
-        deal_weights(nc.scalar.copy, w2_grouped, w2_raw[0], halves[0])
-        deal_weights(nc.scalar.copy, w2_grouped, w2_raw[1], slice(HALF, N - W2_VECTOR), HALF, first)
+        deal_weights(nc.scalar.copy, w2_grouped, w2_raw, slice(0, N), first, first)
+        deal_weights(nc.scalar.copy, w2_grouped, w2_raw, slice(0, N - W2_VECTOR), first, second)
         quantize_rr(0)
-        deal_weights(nc.vector.tensor_copy, w2_grouped, w2_raw[1], slice(N - W2_VECTOR, N), HALF, first)
+        deal_weights(nc.vector.tensor_copy, w2_grouped, w2_raw, slice(N - W2_VECTOR, N), first, second)
         quantize_rr(1)
         w2_mx = [quantize_weights(w2_grouped, "w2", t) for t in range(2)]
-        deal_weights(nc.vector.tensor_copy, w2_grouped, w2_raw[1], halves[1], HALF, second)
+        deal_weights(nc.scalar.copy, w2_grouped, w2_raw, slice(0, HALF), second)
+        deal_weights(nc.vector.tensor_copy, w2_grouped, w2_raw, slice(HALF, N), second)
         w2_mx.extend(quantize_weights(w2_grouped, "w2", t) for t in range(2, PACK))
 
         f_rows = tile([P, PACK * S], F32, "f_rows")

@@ -20,8 +20,9 @@ PACK = 4
 HALF = 256
 QUARTER = 128
 W1_VECTOR = (192, 352)
-W2_VECTOR = 128
+TWO_SETS = 2 * P * PACK
 WIDE = 704
+OPENING = (slice(0, QUARTER), slice(QUARTER, HALF + QUARTER), slice(HALF + QUARTER, 2 * HALF))
 PIECES = (slice(0, HALF), slice(HALF, HALF + QUARTER), slice(HALF + QUARTER, 2 * HALF))
 
 
@@ -59,25 +60,25 @@ def tile_picked_ylbm_str_po_kernel(
         nc.sync.dma_start(out=xw_table[:], in_=x_words[0].rearrange("p n t -> p (n t)").bitcast(I32))
         nc.scalar.activation(keep_sb[:], rate_sb[:], ACT.Copy, bias=1.0, scale=-1.0)
 
-        def deal_weights(copy, grouped, raw, cols, sets=slice(0, PACK), rows=slice(0, PACK)):
+        def deal_weights(copy, grouped, raw, cols, sets=slice(0, PACK), rows=slice(0, PACK), base=0):
             copy(
-                out=grouped[:, sets, cols.start // PACK : cols.stop // PACK, rows].rearrange("p t m j -> p m j t"),
+                out=grouped[:, sets.start - base : sets.stop - base, cols.start // PACK : cols.stop // PACK, rows].rearrange("p t m j -> p m j t"),
                 in_=raw[:, rows, cols].rearrange("p j (m t) -> p m j t", t=PACK)[:, :, :, sets],
             )
 
-        def quantize_weights(grouped, name, t):
+        def quantize_weights(grouped, name, t, base=0):
             codes = tile([P, P], I32, name + "_codes" + str(t))
             scales = tile([P, P], U8, name + "_scales" + str(t))
             nc.vector.quantize_mx(
                 out=codes[:].bitcast(FP8X4),
                 scales=scales[:],
-                in_=grouped[:, t, :, :].rearrange("p m j -> p (m j)"),
+                in_=grouped[:, t - base, :, :].rearrange("p m j -> p (m j)"),
             )
             return codes, scales
 
         def product(bank, weights, codes, scales):
             nc.tensor.matmul_mx(
-                out=bank[:],
+                out=bank,
                 lhsT=weights[0][:].bitcast(FP8X4),
                 lhsT_scale=weights[1][:],
                 rhs=codes.bitcast(FP8X4),
@@ -110,14 +111,12 @@ def tile_picked_ylbm_str_po_kernel(
             deal_weights(nc.scalar.copy, w1_grouped, w1_raw, slice(share, H), rows=pair)
         w1_mx = [quantize_weights(w1_grouped, "w1", t) for t in range(PACK)]
 
-        x_word = []
+        x_word = tile([P, S], I32, "x_word")
         for h in range(2):
-            picked = tile([P, HALF], I32, "x_word" + str(h))
             nc.vector.tensor_copy(
-                picked[:].bitcast(U32),
+                x_word[:, h * HALF : (h + 1) * HALF].bitcast(U32),
                 xw_table[:].bitcast(U32).indirect(offs_sb[:, 16 * h : 16 * (h + 1)]),
             )
-            x_word.append(picked)
 
         halves = [slice(h * HALF, (h + 1) * HALF) for h in range(2)]
         pull = tile([P, PACK, S], F32, "pull")
@@ -133,7 +132,7 @@ def tile_picked_ylbm_str_po_kernel(
             kept = tile([P, PACK, HALF], F32, "kept" + str(h))
             for t in range(PACK):
                 bank = psum.tile([P, HALF], F32, name="bank" + str(PACK * h + t))
-                product(bank, w1_mx[t], x_word[h][:], x_scale[:, cols])
+                product(bank[:], w1_mx[t], x_word[:, cols], x_scale[:, cols])
                 nc.scalar.activation(kept[:, t, :], bank[:], ACT.Copy, scale=keep_sb[:, t : t + 1])
             make_pull(PACK - 1, cols)
             relaxed = tile([P, HALF, PACK], BF16, "rr" + str(h))
@@ -145,6 +144,10 @@ def tile_picked_ylbm_str_po_kernel(
             )
             rr.append(relaxed)
 
+        idle = psum.tile([P, S], F32, name="bank7")
+        for t in range(2):
+            product(idle[:], w1_mx[t], x_word[:], x_scale[:])
+
         rr_codes = tile([P, S], I32, "rr_codes")
         rr_scales = tile([P, S], U8, "rr_scales")
 
@@ -155,31 +158,41 @@ def tile_picked_ylbm_str_po_kernel(
                 in_=rr[h][:].rearrange("p n t -> p (n t)"),
             )
 
-        w2_grouped = tile([P, PACK, P, PACK], BF16, "w2_grouped", "w1_codes3")
-        deal_weights(nc.scalar.copy, w2_grouped, w2_raw, slice(0, N), first, first)
-        deal_weights(nc.scalar.copy, w2_grouped, w2_raw, slice(0, N - W2_VECTOR), first, second)
+        w2_rounded = tile([P, 2 * TWO_SETS - HALF], BF16, "w2_rounded", "w1_codes3")
+        latter = w2_rounded[:, :TWO_SETS].rearrange("p (t m j) -> p t m j", t=2, j=PACK)
+        early = w2_rounded[:, TWO_SETS - HALF :].rearrange("p (t m j) -> p t m j", t=2, j=PACK)
+        for pair in (first, second):
+            deal_weights(nc.scalar.copy, early, w2_raw, slice(0, N), first, pair)
         quantize_rr(0)
-        deal_weights(nc.vector.tensor_copy, w2_grouped, w2_raw, slice(N - W2_VECTOR, N), first, second)
         quantize_rr(1)
-        w2_mx = [quantize_weights(w2_grouped, "w2", t) for t in range(2)]
-        deal_weights(nc.scalar.copy, w2_grouped, w2_raw, slice(0, HALF), second)
-        deal_weights(nc.vector.tensor_copy, w2_grouped, w2_raw, slice(HALF, N), second)
-        w2_mx.extend(quantize_weights(w2_grouped, "w2", t) for t in range(2, PACK))
+        w2_mx = [quantize_weights(early, "w2", t) for t in range(2)]
+        deal_weights(nc.scalar.copy, latter, w2_raw, slice(0, HALF), second, base=2)
+        deal_weights(nc.vector.tensor_copy, latter, w2_raw, slice(HALF, N), second, base=2)
+        w2_mx.append(quantize_weights(latter, "w2", 2, 2))
 
         f_rows = tile([P, PACK * S], F32, "f_rows")
 
         def f_start(t):
             return (PACK - 1 - t) * S
 
-        def populations(i, t, cols):
+        def populations(i, t, cols, width, copy=nc.scalar.copy):
             bank = psum.tile([P, cols.stop - cols.start], F32, name="bank" + str(i))
-            product(bank, w2_mx[t], rr_codes[:, cols], rr_scales[:, cols])
-            nc.scalar.copy(out=f_rows[:, f_start(t) + cols.start : f_start(t) + cols.stop], in_=bank[:])
+            for start in range(cols.start, cols.stop, width):
+                part = slice(start, start + width)
+                product(
+                    bank[:, start - cols.start : start - cols.start + width],
+                    w2_mx[t],
+                    rr_codes[:, part],
+                    rr_scales[:, part],
+                )
+            copy(out=f_rows[:, f_start(t) + cols.start : f_start(t) + cols.stop], in_=bank[:])
 
-        populations(0, 0, halves[0])
-        populations(1, 0, halves[1])
+        populations(0, 0, OPENING[0], QUARTER)
+        populations(1, 0, OPENING[1], QUARTER)
+        populations(2, 0, OPENING[2], QUARTER, nc.vector.tensor_copy)
+        w2_mx.append(quantize_weights(latter, "w2", 3, 2))
         for t in range(1, PACK):
-            populations(1 + t, t, slice(0, S))
+            populations(2 + t, t, slice(0, S), QUARTER if t == 1 else HALF)
 
         out_rows = out_0.rearrange("(p t) n -> p t n", t=PACK)
         out_words = out_1[0].rearrange("p n t -> p (n t)").bitcast(I32)

@@ -19,8 +19,10 @@ P = 128
 PACK = 4
 HALF = 256
 QUARTER = 128
-W1_VECTOR = (192, 352)
+W1_VECTOR = 336
+W2_VECTOR = 192
 TWO_SETS = 2 * P * PACK
+OUT_SCALAR = 64
 WIDE = 704
 OPENING = (slice(0, QUARTER), slice(QUARTER, HALF + QUARTER), slice(HALF + QUARTER, 2 * HALF))
 PIECES = (slice(0, HALF), slice(HALF, HALF + QUARTER), slice(HALF + QUARTER, 2 * HALF))
@@ -54,8 +56,7 @@ def tile_picked_ylbm_str_po_kernel(
         nc.sync.dma_start(out=w1_raw[:, 0:1, :], in_=w1_rows[:, 0:1, :])
         nc.sync.dma_start(offs_sb[:], offs)
         nc.sync.dma_start(out=xs_table[0:P:8, :].bitcast(I32), in_=x_scales[0].bitcast(I32))
-        nc.sync.dma_start(out=w1_raw[:, 1:2, :], in_=w1_rows[:, 1:2, :])
-        nc.sync.dma_start(out=w1_raw[:, second, :], in_=w1_rows[:, second, :])
+        nc.sync.dma_start(out=w1_raw[:, 1:PACK, :], in_=w1_rows[:, 1:PACK, :])
         nc.scalar.dma_start(out=rate_sb[:], in_=rate.rearrange("(p t) o -> p (t o)", t=PACK))
         nc.sync.dma_start(out=xw_table[:], in_=x_words[0].rearrange("p n t -> p (n t)").bitcast(I32))
         nc.scalar.activation(keep_sb[:], rate_sb[:], ACT.Copy, bias=1.0, scale=-1.0)
@@ -106,9 +107,8 @@ def tile_picked_ylbm_str_po_kernel(
         nc.sync.dma_start(src_sb[:], src)
 
         w1_grouped = tile([P, PACK, P, PACK], BF16, "w1_grouped")
-        for pair, share in zip((first, second), W1_VECTOR):
-            deal_weights(nc.vector.tensor_copy, w1_grouped, w1_raw, slice(0, share), rows=pair)
-            deal_weights(nc.scalar.copy, w1_grouped, w1_raw, slice(share, H), rows=pair)
+        deal_weights(nc.vector.tensor_copy, w1_grouped, w1_raw, slice(0, W1_VECTOR))
+        deal_weights(nc.scalar.copy, w1_grouped, w1_raw, slice(W1_VECTOR, H))
         w1_mx = [quantize_weights(w1_grouped, "w1", t) for t in range(PACK)]
 
         x_word = tile([P, S], I32, "x_word")
@@ -158,19 +158,20 @@ def tile_picked_ylbm_str_po_kernel(
                 in_=rr[h][:].rearrange("p n t -> p (n t)"),
             )
 
-        w2_rounded = tile([P, 2 * TWO_SETS - HALF], BF16, "w2_rounded", "w1_codes3")
+        w2_rounded = tile([P, 2 * TWO_SETS - W2_VECTOR], BF16, "w2_rounded", "w1_codes3")
         latter = w2_rounded[:, :TWO_SETS].rearrange("p (t m j) -> p t m j", t=2, j=PACK)
-        early = w2_rounded[:, TWO_SETS - HALF :].rearrange("p (t m j) -> p t m j", t=2, j=PACK)
+        early = w2_rounded[:, TWO_SETS - W2_VECTOR :].rearrange("p (t m j) -> p t m j", t=2, j=PACK)
         for pair in (first, second):
             deal_weights(nc.scalar.copy, early, w2_raw, slice(0, N), first, pair)
         quantize_rr(0)
         quantize_rr(1)
         w2_mx = [quantize_weights(early, "w2", t) for t in range(2)]
-        deal_weights(nc.scalar.copy, latter, w2_raw, slice(0, HALF), second, base=2)
-        deal_weights(nc.vector.tensor_copy, latter, w2_raw, slice(HALF, N), second, base=2)
+        deal_weights(nc.scalar.copy, latter, w2_raw, slice(0, N - W2_VECTOR), second, base=2)
+        deal_weights(nc.vector.tensor_copy, latter, w2_raw, slice(N - W2_VECTOR, N), second, base=2)
         w2_mx.append(quantize_weights(latter, "w2", 2, 2))
 
-        f_rows = tile([P, PACK * S], F32, "f_rows")
+        f_rows = tile([P, PACK * S + WIDE - S], F32, "f_rows")
+        nc.vector.memset(f_rows[:, PACK * S :], 0.0)
 
         def f_start(t):
             return (PACK - 1 - t) * S
@@ -224,8 +225,7 @@ def tile_picked_ylbm_str_po_kernel(
             )
 
         whole = slice(0, S)
-        for cols in halves:
-            stream(0, cols)
+        stream(0, whole, WIDE)
         stream(1, whole, WIDE)
         store(first, whole)
         round_pair(nc.scalar.copy, first, whole)
@@ -235,13 +235,12 @@ def tile_picked_ylbm_str_po_kernel(
             stream(3, cols)
         store(slice(3, PACK), whole)
         round_pair(nc.scalar.copy, second, PIECES[0])
-        round_pair(nc.scalar.copy, second, PIECES[1])
-        quantize_out(PIECES[0])
-        nc.sync.dma_start(out=out_words[:, halves[0]], in_=out_codes[:, halves[0]])
+        round_pair(nc.scalar.copy, second, slice(HALF, HALF + OUT_SCALAR))
+        round_pair(nc.vector.tensor_copy, second, slice(HALF + OUT_SCALAR, PIECES[1].stop))
         round_pair(nc.vector.tensor_copy, second, PIECES[2])
-        quantize_out(PIECES[1])
-        quantize_out(PIECES[2])
-        nc.sync.dma_start(out=out_words[:, halves[1]], in_=out_codes[:, halves[1]])
+        for cols in halves:
+            quantize_out(cols)
+            nc.sync.dma_start(out=out_words[:, cols], in_=out_codes[:, cols])
         for q in range(4):
             queue = nc.sync if q % 2 else nc.scalar
             queue.dma_start(

@@ -19,7 +19,7 @@ P = 128
 PACK = 4
 HALF = 256
 QUARTER = 128
-W1_VECTOR = 336
+W1_VECTOR = (192, 352)
 W2_VECTOR = 192
 TWO_SETS = 2 * P * PACK
 OUT_SCALAR = 64
@@ -56,12 +56,13 @@ def tile_picked_ylbm_str_po_kernel(
         nc.sync.dma_start(out=w1_raw[:, 0:1, :], in_=w1_rows[:, 0:1, :])
         nc.sync.dma_start(offs_sb[:], offs)
         nc.sync.dma_start(out=xs_table[0:P:8, :].bitcast(I32), in_=x_scales[0].bitcast(I32))
-        nc.sync.dma_start(out=w1_raw[:, 1:PACK, :], in_=w1_rows[:, 1:PACK, :])
+        nc.sync.dma_start(out=w1_raw[:, 1:2, :], in_=w1_rows[:, 1:2, :])
+        nc.sync.dma_start(out=w1_raw[:, second, :], in_=w1_rows[:, second, :])
         nc.scalar.dma_start(out=rate_sb[:], in_=rate.rearrange("(p t) o -> p (t o)", t=PACK))
         nc.sync.dma_start(out=xw_table[:], in_=x_words[0].rearrange("p n t -> p (n t)").bitcast(I32))
         nc.scalar.activation(keep_sb[:], rate_sb[:], ACT.Copy, bias=1.0, scale=-1.0)
 
-        def deal_weights(copy, grouped, raw, cols, sets=slice(0, PACK), rows=slice(0, PACK), base=0):
+        def deal_weights(copy, grouped, raw, cols, sets, rows=slice(0, PACK), base=0):
             copy(
                 out=grouped[:, sets.start - base : sets.stop - base, cols.start // PACK : cols.stop // PACK, rows].rearrange("p t m j -> p m j t"),
                 in_=raw[:, rows, cols].rearrange("p j (m t) -> p m j t", t=PACK)[:, :, :, sets],
@@ -107,8 +108,16 @@ def tile_picked_ylbm_str_po_kernel(
         nc.sync.dma_start(src_sb[:], src)
 
         w1_grouped = tile([P, PACK, P, PACK], BF16, "w1_grouped")
-        deal_weights(nc.vector.tensor_copy, w1_grouped, w1_raw, slice(0, W1_VECTOR))
-        deal_weights(nc.scalar.copy, w1_grouped, w1_raw, slice(W1_VECTOR, H))
+
+        def deal_w1(copy, cols, rows):
+            copy(
+                out=w1_grouped[:, :, cols.start // PACK : cols.stop // PACK, rows].rearrange("p (u t) m j -> p u m j t", t=2),
+                in_=w1_raw[:, rows, cols].rearrange("p j (m u t) -> p u m j t", u=2, t=2),
+            )
+
+        for pair, share in zip((first, second), W1_VECTOR):
+            deal_w1(nc.vector.tensor_copy, slice(0, share), pair)
+            deal_w1(nc.scalar.copy, slice(share, H), pair)
         w1_mx = [quantize_weights(w1_grouped, "w1", t) for t in range(PACK)]
 
         x_word = tile([P, S], I32, "x_word")

@@ -64,8 +64,8 @@ def tile_picked_ylbm_str_po_kernel(
 
         def deal_weights(copy, grouped, raw, cols, sets, rows=slice(0, PACK), base=0):
             copy(
-                out=grouped[:, sets.start - base : sets.stop - base, cols.start // PACK : cols.stop // PACK, rows].rearrange("p t m j -> p m j t"),
-                in_=raw[:, rows, cols].rearrange("p j (m t) -> p m j t", t=PACK)[:, :, :, sets],
+                out=grouped[:, sets.start - base : sets.stop - base, cols.start // PACK : cols.stop // PACK, rows].rearrange("p t m j -> p m t j"),
+                in_=raw[:, rows, cols].rearrange("p j (m t) -> p m t j", t=PACK)[:, :, sets, :],
             )
 
         def quantize_weights(grouped, name, t, base=0):
@@ -111,8 +111,8 @@ def tile_picked_ylbm_str_po_kernel(
 
         def deal_w1(copy, cols, rows):
             copy(
-                out=w1_grouped[:, :, cols.start // PACK : cols.stop // PACK, rows].rearrange("p (u t) m j -> p u m j t", t=2),
-                in_=w1_raw[:, rows, cols].rearrange("p j (m u t) -> p u m j t", u=2, t=2),
+                out=w1_grouped[:, :, cols.start // PACK : cols.stop // PACK, rows].rearrange("p (u t) m j -> p u m t j", t=2),
+                in_=w1_raw[:, rows, cols].rearrange("p j (m u t) -> p u m t j", u=2, t=2),
             )
 
         for pair, share in zip((first, second), W1_VECTOR):
@@ -222,8 +222,8 @@ def tile_picked_ylbm_str_po_kernel(
 
         def round_pair(copy, rows, cols):
             copy(
-                out=rounded[:, cols, rows].rearrange("p (c i) t -> p c t i", i=4),
-                in_=streamed[:, rows, cols].rearrange("p t (c i) -> p c t i", i=4),
+                out=rounded[:, cols, rows],
+                in_=streamed[:, rows, cols].rearrange("p t c -> p c t"),
             )
 
         def quantize_out(cols):

@@ -20,7 +20,7 @@ PACK = 4
 HALF = 256
 QUARTER = 128
 W1_VECTOR = (192, 352)
-W2_VECTOR = 192
+W2_VECTOR = 256
 TWO_SETS = 2 * P * PACK
 OUT_SCALAR = 64
 WIDE = 704

@@ -49,9 +49,8 @@ def tile_picked_ylbm_str_po_kernel(
         x_scale = tile([P, S], U8, "x_scale")
 
         first, second = slice(0, 2), slice(2, PACK)
-        nc.vector.memset(xs_table[:, : T // 2].bitcast(I32), 0)
-        nc.gpsimd.memset(xs_table[:, T // 2 :].bitcast(I32), 0)
-        nc.gpsimd.memset(x_scale[:].bitcast(I32), 0)
+        nc.vector.memset(xs_table[:].bitcast(I32), 0)
+        nc.vector.memset(x_scale[:].bitcast(I32), 0)
         w1_rows = w1.rearrange("(p j) c -> p j c", j=PACK)
         nc.sync.dma_start(out=w1_raw[:, 0:1, :], in_=w1_rows[:, 0:1, :])
         nc.sync.dma_start(offs_sb[:], offs)

@@ -22,7 +22,6 @@ QUARTER = 128
 W1_VECTOR = (192, 352)
 W2_VECTOR = 256
 TWO_SETS = 2 * P * PACK
-OUT_SCALAR = 64
 WIDE = 704
 OPENING = (slice(0, QUARTER), slice(QUARTER, HALF + QUARTER), slice(HALF + QUARTER, 2 * HALF))
 PIECES = (slice(0, HALF), slice(HALF, HALF + QUARTER), slice(HALF + QUARTER, 2 * HALF))
@@ -152,10 +151,6 @@ def tile_picked_ylbm_str_po_kernel(
             )
             rr.append(relaxed)
 
-        idle = psum.tile([P, S], F32, name="bank7")
-        for t in range(2):
-            product(idle[:], w1_mx[t], x_word[:], x_scale[:])
-
         rr_codes = tile([P, S], I32, "rr_codes")
         rr_scales = tile([P, S], U8, "rr_scales")
 
@@ -184,24 +179,17 @@ def tile_picked_ylbm_str_po_kernel(
         def f_start(t):
             return (PACK - 1 - t) * S
 
-        def populations(i, t, cols, width, copy=nc.scalar.copy):
+        def populations(i, t, cols, copy=nc.scalar.copy):
             bank = psum.tile([P, cols.stop - cols.start], F32, name="bank" + str(i))
-            for start in range(cols.start, cols.stop, width):
-                part = slice(start, start + width)
-                product(
-                    bank[:, start - cols.start : start - cols.start + width],
-                    w2_mx[t],
-                    rr_codes[:, part],
-                    rr_scales[:, part],
-                )
+            product(bank[:], w2_mx[t], rr_codes[:, cols], rr_scales[:, cols])
             copy(out=f_rows[:, f_start(t) + cols.start : f_start(t) + cols.stop], in_=bank[:])
 
-        populations(0, 0, OPENING[0], QUARTER)
-        populations(1, 0, OPENING[1], QUARTER)
-        populations(2, 0, OPENING[2], QUARTER, nc.vector.tensor_copy)
         w2_mx.append(quantize_weights(latter, "w2", 3, 2))
+        populations(0, 0, OPENING[0])
+        populations(1, 0, OPENING[1])
+        populations(2, 0, OPENING[2], nc.vector.tensor_copy)
         for t in range(1, PACK):
-            populations(2 + t, t, slice(0, S), QUARTER if t == 1 else HALF)
+            populations(2 + t, t, slice(0, S))
 
         out_rows = out_0.rearrange("(p t) n -> p t n", t=PACK)
         out_words = out_1[0].rearrange("p n t -> p (n t)").bitcast(I32)
@@ -243,12 +231,13 @@ def tile_picked_ylbm_str_po_kernel(
             stream(3, cols)
         store(slice(3, PACK), whole)
         round_pair(nc.scalar.copy, second, PIECES[0])
-        round_pair(nc.scalar.copy, second, slice(HALF, HALF + OUT_SCALAR))
-        round_pair(nc.vector.tensor_copy, second, slice(HALF + OUT_SCALAR, PIECES[1].stop))
+        round_pair(nc.vector.tensor_copy, second, PIECES[1])
         round_pair(nc.vector.tensor_copy, second, PIECES[2])
-        for cols in halves:
-            quantize_out(cols)
-            nc.sync.dma_start(out=out_words[:, cols], in_=out_codes[:, cols])
+        quantize_out(PIECES[1])
+        quantize_out(PIECES[2])
+        nc.sync.dma_start(out=out_words[:, halves[1]], in_=out_codes[:, halves[1]])
+        quantize_out(PIECES[0])
+        nc.sync.dma_start(out=out_words[:, halves[0]], in_=out_codes[:, halves[0]])
         for q in range(4):
             queue = nc.sync if q % 2 else nc.scalar
             queue.dma_start(

@@ -20,7 +20,7 @@ PACK = 4
 HALF = 256
 QUARTER = 128
 W1_VECTOR = (192, 352)
-W2_VECTOR = 256
+W2_VECTOR = 192
 TWO_SETS = 2 * P * PACK
 WIDE = 704
 OPENING = (slice(0, QUARTER), slice(QUARTER, HALF + QUARTER), slice(HALF + QUARTER, 2 * HALF))
@@ -74,13 +74,13 @@ def tile_picked_ylbm_str_po_kernel(
                 scales=scales[:],
                 in_=grouped[:, t - base, :, :].rearrange("p m j -> p (m j)"),
             )
-            return codes, scales
+            return codes[:], scales[:]
 
         def product(bank, weights, codes, scales):
             nc.tensor.matmul_mx(
                 out=bank,
-                lhsT=weights[0][:].bitcast(FP8X4),
-                lhsT_scale=weights[1][:],
+                lhsT=weights[0].bitcast(FP8X4),
+                lhsT_scale=weights[1],
                 rhs=codes.bitcast(FP8X4),
                 rhs_scale=scales,
                 start=True,
@@ -116,7 +116,15 @@ def tile_picked_ylbm_str_po_kernel(
         for pair, share in zip((first, second), W1_VECTOR):
             deal_w1(nc.vector.tensor_copy, slice(0, share), pair)
             deal_w1(nc.scalar.copy, slice(share, H), pair)
-        w1_mx = [quantize_weights(w1_grouped, "w1", t) for t in range(PACK)]
+        w1_codes = tile([P, H], I32, "w1_codes")
+        w1_scales = tile([P, H], U8, "w1_scales")
+        w1_mx = [(w1_codes[:, t * P : (t + 1) * P], w1_scales[:, t * P : (t + 1) * P]) for t in range(PACK)]
+        for t in range(PACK):
+            nc.vector.quantize_mx(
+                out=w1_mx[t][0].bitcast(FP8X4),
+                scales=w1_mx[t][1],
+                in_=w1_grouped[:, t, :, :].rearrange("p m j -> p (m j)"),
+            )
 
         x_word = tile([P, S], I32, "x_word")
         for h in range(2):
@@ -161,7 +169,7 @@ def tile_picked_ylbm_str_po_kernel(
                 in_=rr[h][:].rearrange("p n t -> p (n t)"),
             )
 
-        w2_rounded = tile([P, 2 * TWO_SETS - W2_VECTOR], BF16, "w2_rounded", "w1_codes3")
+        w2_rounded = tile([P, 2 * TWO_SETS - W2_VECTOR], BF16, "w2_rounded", "x_word")
         latter = w2_rounded[:, :TWO_SETS].rearrange("p (t m j) -> p t m j", t=2, j=PACK)
         early = w2_rounded[:, TWO_SETS - W2_VECTOR :].rearrange("p (t m j) -> p t m j", t=2, j=PACK)
         for pair in (first, second):
@@ -184,10 +192,10 @@ def tile_picked_ylbm_str_po_kernel(
             product(bank[:], w2_mx[t], rr_codes[:, cols], rr_scales[:, cols])
             copy(out=f_rows[:, f_start(t) + cols.start : f_start(t) + cols.stop], in_=bank[:])
 
-        w2_mx.append(quantize_weights(latter, "w2", 3, 2))
         populations(0, 0, OPENING[0])
         populations(1, 0, OPENING[1])
         populations(2, 0, OPENING[2], nc.vector.tensor_copy)
+        w2_mx.append(quantize_weights(latter, "w2", 3, 2))
         for t in range(1, PACK):
             populations(2 + t, t, slice(0, S))
 

@@ -23,6 +23,7 @@ W1_VECTOR = (192, 352)
 W2_VECTOR = 192
 TWO_SETS = 2 * P * PACK
 WIDE = 704
+WARM = 32
 OPENING = (slice(0, QUARTER), slice(QUARTER, HALF + QUARTER), slice(HALF + QUARTER, 2 * HALF))
 PIECES = (slice(0, HALF), slice(HALF, HALF + QUARTER), slice(HALF + QUARTER, 2 * HALF))
 
@@ -159,6 +160,11 @@ def tile_picked_ylbm_str_po_kernel(
             )
             rr.append(relaxed)
 
+        idle = psum.tile([WARM, H], F32, name="bank7")
+        for start in (0, P):
+            narrow = slice(start, start + WARM)
+            product(idle[:], (w1_codes[:, narrow], w1_scales[:, narrow]), w1_codes[:], w1_scales[:])
+
         rr_codes = tile([P, S], I32, "rr_codes")
         rr_scales = tile([P, S], U8, "rr_scales")
 
@@ -175,6 +181,7 @@ def tile_picked_ylbm_str_po_kernel(
         for pair in (first, second):
             deal_weights(nc.scalar.copy, early, w2_raw, slice(0, N), first, pair)
         quantize_rr(0)
+        product(idle[:], (rr_codes[:, :WARM], rr_scales[:, :WARM]), w1_codes[:], w1_scales[:])
         quantize_rr(1)
         w2_mx = [quantize_weights(early, "w2", t) for t in range(2)]
         deal_weights(nc.scalar.copy, latter, w2_raw, slice(0, N - W2_VECTOR), second, base=2)

@@ -19,13 +19,17 @@ P = 128
 PACK = 4
 HALF = 256
 QUARTER = 128
-W1_VECTOR = (192, 352)
-W2_VECTOR = 192
+WHOLE = slice(0, S)
+LOW, HIGH = slice(0, HALF), slice(HALF, S)
+THIRD, FOURTH = slice(HALF, HALF + QUARTER), slice(HALF + QUARTER, S)
+FRONT, BACK = slice(0, 2), slice(2, PACK)
 TWO_SETS = 2 * P * PACK
+
+W1_VECTOR = (192, 352)
+W2_VECTOR = 256
 WIDE = 704
+OPENING = (slice(0, QUARTER), slice(QUARTER, HALF + QUARTER), FOURTH)
 WARM = 32
-OPENING = (slice(0, QUARTER), slice(QUARTER, HALF + QUARTER), slice(HALF + QUARTER, 2 * HALF))
-PIECES = (slice(0, HALF), slice(HALF, HALF + QUARTER), slice(HALF + QUARTER, 2 * HALF))
 
 
 def tile_picked_ylbm_str_po_kernel(
@@ -39,6 +43,23 @@ def tile_picked_ylbm_str_po_kernel(
         def tile(shape, dtype, name, tag=None):
             return sb.tile(shape, dtype, name=name, tag=tag or name, align_bytes=64)
 
+        def offsets(list_tile, cols):
+            return list_tile[:, cols.start // 16 : cols.stop // 16]
+
+        def quantize(codes, scales, values):
+            nc.vector.quantize_mx(out=codes.bitcast(FP8X4), scales=scales, in_=values)
+
+        def product(bank, stationary, codes, scales):
+            nc.tensor.matmul_mx(
+                out=bank,
+                lhsT=stationary[0].bitcast(FP8X4),
+                lhsT_scale=stationary[1],
+                rhs=codes.bitcast(FP8X4),
+                rhs_scale=scales,
+                start=True,
+                stop=True,
+            )
+
         offs_sb = tile([P, S // 16], U16, "offs_sb")
         src_sb = tile([P, S // 16], U16, "src_sb")
         xs_table = tile([P, T], U8, "xs_table")
@@ -48,45 +69,18 @@ def tile_picked_ylbm_str_po_kernel(
         w1_raw = tile([P, PACK, H], F32, "w1_raw")
         x_scale = tile([P, S], U8, "x_scale")
 
-        first, second = slice(0, 2), slice(2, PACK)
         nc.vector.memset(xs_table[:].bitcast(I32), 0)
         nc.vector.memset(x_scale[:].bitcast(I32), 0)
+
         w1_rows = w1.rearrange("(p j) c -> p j c", j=PACK)
         nc.sync.dma_start(out=w1_raw[:, 0:1, :], in_=w1_rows[:, 0:1, :])
         nc.sync.dma_start(offs_sb[:], offs)
         nc.sync.dma_start(out=xs_table[0:P:8, :].bitcast(I32), in_=x_scales[0].bitcast(I32))
         nc.sync.dma_start(out=w1_raw[:, 1:2, :], in_=w1_rows[:, 1:2, :])
-        nc.sync.dma_start(out=w1_raw[:, second, :], in_=w1_rows[:, second, :])
+        nc.sync.dma_start(out=w1_raw[:, BACK, :], in_=w1_rows[:, BACK, :])
         nc.scalar.dma_start(out=rate_sb[:], in_=rate.rearrange("(p t) o -> p (t o)", t=PACK))
         nc.sync.dma_start(out=xw_table[:], in_=x_words[0].rearrange("p n t -> p (n t)").bitcast(I32))
         nc.scalar.activation(keep_sb[:], rate_sb[:], ACT.Copy, bias=1.0, scale=-1.0)
-
-        def deal_weights(copy, grouped, raw, cols, sets, rows=slice(0, PACK), base=0):
-            copy(
-                out=grouped[:, sets.start - base : sets.stop - base, cols.start // PACK : cols.stop // PACK, rows].rearrange("p t m j -> p m t j"),
-                in_=raw[:, rows, cols].rearrange("p j (m t) -> p m t j", t=PACK)[:, :, sets, :],
-            )
-
-        def quantize_weights(grouped, name, t, base=0):
-            codes = tile([P, P], I32, name + "_codes" + str(t))
-            scales = tile([P, P], U8, name + "_scales" + str(t))
-            nc.vector.quantize_mx(
-                out=codes[:].bitcast(FP8X4),
-                scales=scales[:],
-                in_=grouped[:, t - base, :, :].rearrange("p m j -> p (m j)"),
-            )
-            return codes[:], scales[:]
-
-        def product(bank, weights, codes, scales):
-            nc.tensor.matmul_mx(
-                out=bank,
-                lhsT=weights[0].bitcast(FP8X4),
-                lhsT_scale=weights[1],
-                rhs=codes.bitcast(FP8X4),
-                rhs_scale=scales,
-                start=True,
-                stop=True,
-            )
 
         xs_picked = tile([P, S], U8, "xs_picked")
         nc.vector.tensor_copy(xs_picked[:], xs_table[:].indirect(offs_sb[:]))
@@ -95,15 +89,16 @@ def tile_picked_ylbm_str_po_kernel(
                 out=x_scale[32 * q : 32 * q + 4, :].bitcast(I32),
                 in_=xs_picked[32 * q : 32 * (q + 1) : 8, :].bitcast(I32),
             )
+
         late = tile([P, 2 * PACK * S], F32, "late", "xs_table")
         eq_raw = late[:, : PACK * S].rearrange("p (t c) -> p t c", t=PACK)
         w2_raw = late[:, PACK * S :].rearrange("p (j c) -> p j c", j=PACK)
         eq_rows = eq.rearrange("(p t) c -> p t c", t=PACK)
-        for sets in (slice(0, 2), slice(2, 3), slice(3, PACK)):
+        for sets in (FRONT, slice(2, 3), slice(3, PACK)):
             nc.sync.dma_start(out=eq_raw[:, sets, :], in_=eq_rows[:, sets, :])
         w2_rows = w2.rearrange("(p j) c -> p j c", j=PACK)
-        for pair in (first, second):
-            nc.sync.dma_start(out=w2_raw[:, pair, :], in_=w2_rows[:, pair, :])
+        for rows in (FRONT, BACK):
+            nc.sync.dma_start(out=w2_raw[:, rows, :], in_=w2_rows[:, rows, :])
         nc.sync.dma_start(src_sb[:], src)
 
         w1_grouped = tile([P, PACK, P, PACK], BF16, "w1_grouped")
@@ -114,51 +109,43 @@ def tile_picked_ylbm_str_po_kernel(
                 in_=w1_raw[:, rows, cols].rearrange("p j (m u t) -> p u m t j", u=2, t=2),
             )
 
-        for pair, share in zip((first, second), W1_VECTOR):
-            deal_w1(nc.vector.tensor_copy, slice(0, share), pair)
-            deal_w1(nc.scalar.copy, slice(share, H), pair)
+        for rows, share in zip((FRONT, BACK), W1_VECTOR):
+            deal_w1(nc.vector.tensor_copy, slice(0, share), rows)
+            deal_w1(nc.scalar.copy, slice(share, H), rows)
         w1_codes = tile([P, H], I32, "w1_codes")
         w1_scales = tile([P, H], U8, "w1_scales")
         w1_mx = [(w1_codes[:, t * P : (t + 1) * P], w1_scales[:, t * P : (t + 1) * P]) for t in range(PACK)]
         for t in range(PACK):
-            nc.vector.quantize_mx(
-                out=w1_mx[t][0].bitcast(FP8X4),
-                scales=w1_mx[t][1],
-                in_=w1_grouped[:, t, :, :].rearrange("p m j -> p (m j)"),
-            )
+            quantize(w1_mx[t][0], w1_mx[t][1], w1_grouped[:, t, :, :].rearrange("p m j -> p (m j)"))
 
         x_word = tile([P, S], I32, "x_word")
-        for h in range(2):
-            nc.vector.tensor_copy(
-                x_word[:, h * HALF : (h + 1) * HALF].bitcast(U32),
-                xw_table[:].bitcast(U32).indirect(offs_sb[:, 16 * h : 16 * (h + 1)]),
-            )
+        for cols in (LOW, HIGH):
+            nc.vector.tensor_copy(x_word[:, cols].bitcast(U32), xw_table[:].bitcast(U32).indirect(offsets(offs_sb, cols)))
 
-        halves = [slice(h * HALF, (h + 1) * HALF) for h in range(2)]
         pull = tile([P, PACK, S], F32, "pull")
 
         def make_pull(t, cols):
             nc.vector.tensor_scalar(pull[:, t, cols], eq_raw[:, t, cols], rate_sb[:, t : t + 1], None, ALU.mult)
 
         for t in range(PACK - 1):
-            make_pull(t, slice(0, S))
+            make_pull(t, WHOLE)
 
-        rr = []
-        for h, cols in enumerate(halves):
+        relaxed = []
+        for h, cols in enumerate((LOW, HIGH)):
             kept = tile([P, PACK, HALF], F32, "kept" + str(h))
             for t in range(PACK):
                 bank = psum.tile([P, HALF], F32, name="bank" + str(PACK * h + t))
                 product(bank[:], w1_mx[t], x_word[:, cols], x_scale[:, cols])
                 nc.scalar.activation(kept[:, t, :], bank[:], ACT.Copy, scale=keep_sb[:, t : t + 1])
             make_pull(PACK - 1, cols)
-            relaxed = tile([P, HALF, PACK], BF16, "rr" + str(h))
+            woven = tile([P, HALF, PACK], BF16, "rr" + str(h))
             nc.vector.tensor_tensor(
-                relaxed[:].rearrange("p (c i) t -> p c t i", i=4),
+                woven[:].rearrange("p (c i) t -> p c t i", i=4),
                 kept[:].rearrange("p t (c i) -> p c t i", i=4),
                 pull[:, :, cols].rearrange("p t (c i) -> p c t i", i=4),
                 ALU.add,
             )
-            rr.append(relaxed)
+            relaxed.append(woven)
 
         idle = psum.tile([WARM, H], F32, name="bank7")
         for start in (0, P):
@@ -168,25 +155,34 @@ def tile_picked_ylbm_str_po_kernel(
         rr_codes = tile([P, S], I32, "rr_codes")
         rr_scales = tile([P, S], U8, "rr_scales")
 
-        def quantize_rr(h):
-            nc.vector.quantize_mx(
-                out=rr_codes[:, halves[h]].bitcast(FP8X4),
-                scales=rr_scales[:, halves[h]],
-                in_=rr[h][:].rearrange("p n t -> p (n t)"),
-            )
+        def quantize_rr(h, cols):
+            quantize(rr_codes[:, cols], rr_scales[:, cols], relaxed[h][:].rearrange("p n t -> p (n t)"))
 
         w2_rounded = tile([P, 2 * TWO_SETS - W2_VECTOR], BF16, "w2_rounded", "x_word")
-        latter = w2_rounded[:, :TWO_SETS].rearrange("p (t m j) -> p t m j", t=2, j=PACK)
-        early = w2_rounded[:, TWO_SETS - W2_VECTOR :].rearrange("p (t m j) -> p t m j", t=2, j=PACK)
-        for pair in (first, second):
-            deal_weights(nc.scalar.copy, early, w2_raw, slice(0, N), first, pair)
-        quantize_rr(0)
+        w2_back = w2_rounded[:, :TWO_SETS].rearrange("p (t m j) -> p t m j", t=2, j=PACK)
+        w2_front = w2_rounded[:, TWO_SETS - W2_VECTOR :].rearrange("p (t m j) -> p t m j", t=2, j=PACK)
+
+        def deal_w2(copy, grouped, sets, cols, rows):
+            copy(
+                out=grouped[:, :, cols.start // PACK : cols.stop // PACK, rows].rearrange("p t m j -> p m t j"),
+                in_=w2_raw[:, rows, cols].rearrange("p j (m t) -> p m t j", t=PACK)[:, :, sets, :],
+            )
+
+        def quantize_w2(grouped, t):
+            codes = tile([P, P], I32, "w2_codes" + str(t))
+            scales = tile([P, P], U8, "w2_scales" + str(t))
+            quantize(codes[:], scales[:], grouped[:, t % 2, :, :].rearrange("p m j -> p (m j)"))
+            return codes[:], scales[:]
+
+        for rows in (FRONT, BACK):
+            deal_w2(nc.scalar.copy, w2_front, FRONT, slice(0, N), rows)
+        quantize_rr(0, LOW)
         product(idle[:], (rr_codes[:, :WARM], rr_scales[:, :WARM]), w1_codes[:], w1_scales[:])
-        quantize_rr(1)
-        w2_mx = [quantize_weights(early, "w2", t) for t in range(2)]
-        deal_weights(nc.scalar.copy, latter, w2_raw, slice(0, N - W2_VECTOR), second, base=2)
-        deal_weights(nc.vector.tensor_copy, latter, w2_raw, slice(N - W2_VECTOR, N), second, base=2)
-        w2_mx.append(quantize_weights(latter, "w2", 2, 2))
+        quantize_rr(1, HIGH)
+        w2_mx = [quantize_w2(w2_front, t) for t in range(2)]
+        deal_w2(nc.scalar.copy, w2_back, BACK, slice(0, N - W2_VECTOR), slice(0, PACK))
+        deal_w2(nc.vector.tensor_copy, w2_back, BACK, slice(N - W2_VECTOR, N), slice(0, PACK))
+        w2_mx.append(quantize_w2(w2_back, 2))
 
         f_rows = tile([P, PACK * S + WIDE - S], F32, "f_rows")
         nc.vector.memset(f_rows[:, PACK * S :], 0.0)
@@ -194,17 +190,16 @@ def tile_picked_ylbm_str_po_kernel(
         def f_start(t):
             return (PACK - 1 - t) * S
 
-        def populations(i, t, cols, copy=nc.scalar.copy):
-            bank = psum.tile([P, cols.stop - cols.start], F32, name="bank" + str(i))
+        def populations(bank_number, t, cols, copy):
+            bank = psum.tile([P, cols.stop - cols.start], F32, name="bank" + str(bank_number))
             product(bank[:], w2_mx[t], rr_codes[:, cols], rr_scales[:, cols])
             copy(out=f_rows[:, f_start(t) + cols.start : f_start(t) + cols.stop], in_=bank[:])
 
-        populations(0, 0, OPENING[0])
-        populations(1, 0, OPENING[1])
-        populations(2, 0, OPENING[2], nc.vector.tensor_copy)
-        w2_mx.append(quantize_weights(latter, "w2", 3, 2))
+        for bank_number, copy in enumerate((nc.scalar.copy, nc.scalar.copy, nc.vector.tensor_copy)):
+            populations(bank_number, 0, OPENING[bank_number], copy)
+        w2_mx.append(quantize_w2(w2_back, 3))
         for t in range(1, PACK):
-            populations(2 + t, t, slice(0, S))
+            populations(len(OPENING) - 1 + t, t, WHOLE, nc.scalar.copy)
 
         out_rows = out_0.rearrange("(p t) n -> p t n", t=PACK)
         out_words = out_1[0].rearrange("p n t -> p (n t)").bitcast(I32)
@@ -213,46 +208,38 @@ def tile_picked_ylbm_str_po_kernel(
         streamed = tile([P, PACK, S], F32, "streamed")
         rounded = tile([P, S, PACK], BF16, "rounded")
 
-        def stream(t, cols, window=S):
+        def stream(t, cols, window):
             nc.vector.tensor_copy(
                 streamed[:, t, cols],
-                f_rows[:, f_start(t) : f_start(t) + window].indirect(src_sb[:, cols.start // 16 : cols.stop // 16]),
+                f_rows[:, f_start(t) : f_start(t) + window].indirect(offsets(src_sb, cols)),
             )
 
-        def store(rows, cols):
-            nc.sync.dma_start(out=out_rows[:, rows, cols], in_=streamed[:, rows, cols])
+        def store(sets):
+            nc.sync.dma_start(out=out_rows[:, sets, :], in_=streamed[:, sets, :])
 
-        def round_pair(copy, rows, cols):
-            copy(
-                out=rounded[:, cols, rows],
-                in_=streamed[:, rows, cols].rearrange("p t c -> p c t"),
-            )
+        def weave_pair(copy, sets, cols):
+            copy(out=rounded[:, cols, sets], in_=streamed[:, sets, cols].rearrange("p t c -> p c t"))
 
         def quantize_out(cols):
-            nc.vector.quantize_mx(
-                out=out_codes[:, cols].bitcast(FP8X4),
-                scales=out_scales[:, cols],
-                in_=rounded[:, cols, :].rearrange("p n t -> p (n t)"),
-            )
+            quantize(out_codes[:, cols], out_scales[:, cols], rounded[:, cols, :].rearrange("p n t -> p (n t)"))
 
-        whole = slice(0, S)
-        stream(0, whole, WIDE)
-        stream(1, whole, WIDE)
-        store(first, whole)
-        round_pair(nc.scalar.copy, first, whole)
-        stream(2, whole, WIDE)
-        store(slice(2, 3), whole)
-        for cols in PIECES:
-            stream(3, cols)
-        store(slice(3, PACK), whole)
-        round_pair(nc.scalar.copy, second, PIECES[0])
-        round_pair(nc.vector.tensor_copy, second, PIECES[1])
-        round_pair(nc.vector.tensor_copy, second, PIECES[2])
-        quantize_out(PIECES[1])
-        quantize_out(PIECES[2])
-        nc.sync.dma_start(out=out_words[:, halves[1]], in_=out_codes[:, halves[1]])
-        quantize_out(PIECES[0])
-        nc.sync.dma_start(out=out_words[:, halves[0]], in_=out_codes[:, halves[0]])
+        stream(0, WHOLE, WIDE)
+        stream(1, WHOLE, WIDE)
+        store(FRONT)
+        weave_pair(nc.scalar.copy, FRONT, WHOLE)
+        stream(2, WHOLE, WIDE)
+        store(slice(2, 3))
+        for cols in (LOW, THIRD, FOURTH):
+            stream(3, cols, S)
+        store(slice(3, PACK))
+        weave_pair(nc.scalar.copy, BACK, LOW)
+        for cols in (THIRD, FOURTH):
+            weave_pair(nc.vector.tensor_copy, BACK, cols)
+        for cols in (THIRD, FOURTH):
+            quantize_out(cols)
+        nc.sync.dma_start(out=out_words[:, HIGH], in_=out_codes[:, HIGH])
+        quantize_out(LOW)
+        nc.sync.dma_start(out=out_words[:, LOW], in_=out_codes[:, LOW])
         for q in range(4):
             queue = nc.sync if q % 2 else nc.scalar
             queue.dma_start(

@@ -21,7 +21,8 @@ HALF = 256
 QUARTER = 128
 WHOLE = slice(0, S)
 LOW, HIGH = slice(0, HALF), slice(HALF, S)
-THIRD, FOURTH = slice(HALF, HALF + QUARTER), slice(HALF + QUARTER, S)
+QUARTERS = [slice(q * QUARTER, (q + 1) * QUARTER) for q in range(4)]
+THIRD, FOURTH = QUARTERS[2:]
 FRONT, BACK = slice(0, 2), slice(2, PACK)
 TWO_SETS = 2 * P * PACK
 
@@ -208,8 +209,14 @@ def tile_picked_ylbm_str_po_kernel(
         streamed = tile([P, PACK, S], F32, "streamed")
         rounded = tile([P, S, PACK], BF16, "rounded")
 
-        def stream(t, cols, window):
-            nc.vector.tensor_copy(
+        def gather_on_scalar(out, in_):
+            nc.scalar.activation(out, in_, ACT.Copy)
+
+        def round_on_gpsimd(out, in_):
+            nc.gpsimd.tensor_scalar(out, in_, 1.0, 0.0, ALU.mult, ALU.add)
+
+        def stream(gather, t, cols, window):
+            gather(
                 streamed[:, t, cols],
                 f_rows[:, f_start(t) : f_start(t) + window].indirect(offsets(src_sb, cols)),
             )
@@ -218,28 +225,34 @@ def tile_picked_ylbm_str_po_kernel(
             nc.sync.dma_start(out=out_rows[:, sets, :], in_=streamed[:, sets, :])
 
         def weave_pair(copy, sets, cols):
-            copy(out=rounded[:, cols, sets], in_=streamed[:, sets, cols].rearrange("p t c -> p c t"))
+            copy(rounded[:, cols, sets], streamed[:, sets, cols].rearrange("p t c -> p c t"))
 
         def quantize_out(cols):
             quantize(out_codes[:, cols], out_scales[:, cols], rounded[:, cols, :].rearrange("p n t -> p (n t)"))
 
-        stream(0, WHOLE, WIDE)
-        stream(1, WHOLE, WIDE)
+        stream(nc.vector.tensor_copy, 0, WHOLE, WIDE)
+        stream(nc.vector.tensor_copy, 1, WHOLE, WIDE)
         store(FRONT)
-        weave_pair(nc.scalar.copy, FRONT, WHOLE)
-        stream(2, WHOLE, WIDE)
+        for cols in (LOW, THIRD):
+            weave_pair(round_on_gpsimd, FRONT, cols)
+        stream(nc.vector.tensor_copy, 2, LOW, S)
+        stream(gather_on_scalar, 2, HIGH, S)
         store(slice(2, 3))
-        for cols in (LOW, THIRD, FOURTH):
-            stream(3, cols, S)
+        stream(gather_on_scalar, 3, FOURTH, S)
+        for cols in QUARTERS[:3]:
+            stream(nc.vector.tensor_copy, 3, cols, S)
+            weave_pair(nc.scalar.copy, BACK, cols)
         store(slice(3, PACK))
-        weave_pair(nc.scalar.copy, BACK, LOW)
-        for cols in (THIRD, FOURTH):
-            weave_pair(nc.vector.tensor_copy, BACK, cols)
-        for cols in (THIRD, FOURTH):
+        nc.vector.tensor_copy(
+            rounded[:, FOURTH, :].rearrange("p (c i) t -> p c t i", i=4),
+            streamed[:, :, FOURTH].rearrange("p t (c i) -> p c t i", i=4),
+        )
+        for cols in QUARTERS[:2]:
+            quantize_out(cols)
+        nc.sync.dma_start(out=out_words[:, LOW], in_=out_codes[:, LOW])
+        for cols in (FOURTH, THIRD):
             quantize_out(cols)
         nc.sync.dma_start(out=out_words[:, HIGH], in_=out_codes[:, HIGH])
-        quantize_out(LOW)
-        nc.sync.dma_start(out=out_words[:, LOW], in_=out_codes[:, LOW])
         for q in range(4):
             queue = nc.sync if q % 2 else nc.scalar
             queue.dma_start(

@@ -21,8 +21,7 @@ HALF = 256
 QUARTER = 128
 WHOLE = slice(0, S)
 LOW, HIGH = slice(0, HALF), slice(HALF, S)
-QUARTERS = [slice(q * QUARTER, (q + 1) * QUARTER) for q in range(4)]
-THIRD, FOURTH = QUARTERS[2:]
+FIRST, SECOND, THIRD, FOURTH = [slice(q * QUARTER, (q + 1) * QUARTER) for q in range(4)]
 FRONT, BACK = slice(0, 2), slice(2, PACK)
 TWO_SETS = 2 * P * PACK
 
@@ -230,29 +229,35 @@ def tile_picked_ylbm_str_po_kernel(
         def quantize_out(cols):
             quantize(out_codes[:, cols], out_scales[:, cols], rounded[:, cols, :].rearrange("p n t -> p (n t)"))
 
+        def weave_all(copy, cols):
+            copy(
+                rounded[:, cols, :].rearrange("p (c i) t -> p c t i", i=4),
+                streamed[:, :, cols].rearrange("p t (c i) -> p c t i", i=4),
+            )
+
         stream(nc.vector.tensor_copy, 0, WHOLE, WIDE)
-        stream(nc.vector.tensor_copy, 1, WHOLE, WIDE)
+        for cols in (LOW, HIGH):
+            stream(nc.vector.tensor_copy, 1, cols, S)
         store(FRONT)
-        for cols in (LOW, THIRD):
-            weave_pair(round_on_gpsimd, FRONT, cols)
-        stream(nc.vector.tensor_copy, 2, LOW, S)
-        stream(gather_on_scalar, 2, HIGH, S)
+        weave_pair(round_on_gpsimd, FRONT, LOW)
+        stream(gather_on_scalar, 2, THIRD, S)
+        for cols in (LOW, FOURTH):
+            stream(nc.vector.tensor_copy, 2, cols, S)
         store(slice(2, 3))
-        stream(gather_on_scalar, 3, FOURTH, S)
-        for cols in QUARTERS[:3]:
-            stream(nc.vector.tensor_copy, 3, cols, S)
-            weave_pair(nc.scalar.copy, BACK, cols)
+        for cols in (THIRD, FIRST, SECOND):
+            stream(gather_on_scalar, 3, cols, S)
+        stream(nc.vector.tensor_copy, 3, FOURTH, S)
         store(slice(3, PACK))
-        nc.vector.tensor_copy(
-            rounded[:, FOURTH, :].rearrange("p (c i) t -> p c t i", i=4),
-            streamed[:, :, FOURTH].rearrange("p t (c i) -> p c t i", i=4),
-        )
-        for cols in QUARTERS[:2]:
-            quantize_out(cols)
-        nc.sync.dma_start(out=out_words[:, LOW], in_=out_codes[:, LOW])
-        for cols in (FOURTH, THIRD):
+        weave_pair(round_on_gpsimd, slice(0, PACK), THIRD)
+        weave_all(nc.vector.tensor_copy, FOURTH)
+        for cols in (FIRST, SECOND):
+            weave_pair(nc.scalar.copy, BACK, cols)
+        for cols in (THIRD, FOURTH):
             quantize_out(cols)
         nc.sync.dma_start(out=out_words[:, HIGH], in_=out_codes[:, HIGH])
+        for cols in (FIRST, SECOND):
+            quantize_out(cols)
+        nc.sync.dma_start(out=out_words[:, LOW], in_=out_codes[:, LOW])
         for q in range(4):
             queue = nc.sync if q % 2 else nc.scalar
             queue.dma_start(

@@ -236,9 +236,10 @@ def tile_picked_ylbm_str_po_kernel(
             )
 
         stream(nc.vector.tensor_copy, 0, WHOLE, WIDE)
+        store(slice(0, 1))
         for cols in (LOW, HIGH):
             stream(nc.vector.tensor_copy, 1, cols, S)
-        store(FRONT)
+        store(slice(1, 2))
         weave_pair(round_on_gpsimd, FRONT, LOW)
         stream(gather_on_scalar, 2, THIRD, S)
         for cols in (LOW, FOURTH):

@@ -258,7 +258,7 @@ def tile_picked_ylbm_str_po_kernel(
         nc.sync.dma_start(out=out_words[:, HIGH], in_=out_codes[:, HIGH])
         for cols in (FIRST, SECOND):
             quantize_out(cols)
-        nc.sync.dma_start(out=out_words[:, LOW], in_=out_codes[:, LOW])
+        nc.scalar.dma_start(out=out_words[:, LOW], in_=out_codes[:, LOW])
         for q in range(4):
             queue = nc.sync if q % 2 else nc.scalar
             queue.dma_start(

@@ -119,7 +119,7 @@ def tile_picked_ylbm_str_po_kernel(
             quantize(w1_mx[t][0], w1_mx[t][1], w1_grouped[:, t, :, :].rearrange("p m j -> p (m j)"))
 
         x_word = tile([P, S], I32, "x_word")
-        for cols in (LOW, HIGH):
+        for cols in (FIRST, SECOND, HIGH):
             nc.vector.tensor_copy(x_word[:, cols].bitcast(U32), xw_table[:].bitcast(U32).indirect(offsets(offs_sb, cols)))
 
         pull = tile([P, PACK, S], F32, "pull")
@@ -130,22 +130,30 @@ def tile_picked_ylbm_str_po_kernel(
         for t in range(PACK - 1):
             make_pull(t, WHOLE)
 
-        relaxed = []
-        for h, cols in enumerate((LOW, HIGH)):
-            kept = tile([P, PACK, HALF], F32, "kept" + str(h))
-            for t in range(PACK):
-                bank = psum.tile([P, HALF], F32, name="bank" + str(PACK * h + t))
-                product(bank[:], w1_mx[t], x_word[:, cols], x_scale[:, cols])
-                nc.scalar.activation(kept[:, t, :], bank[:], ACT.Copy, scale=keep_sb[:, t : t + 1])
-            make_pull(PACK - 1, cols)
-            woven = tile([P, HALF, PACK], BF16, "rr" + str(h))
+        relaxed = [tile([P, HALF, PACK], BF16, "rr" + str(h)) for h in range(2)]
+        kept = tile([P, PACK, S], F32, "kept")
+
+        def scale_y(t, cols, bank):
+            nc.scalar.activation(kept[:, t, cols], bank, ACT.Copy, scale=keep_sb[:, t : t + 1])
+
+        def relax(woven, cols):
             nc.vector.tensor_tensor(
-                woven[:].rearrange("p (c i) t -> p c t i", i=4),
-                kept[:].rearrange("p t (c i) -> p c t i", i=4),
+                woven.rearrange("p (c i) t -> p c t i", i=4),
+                kept[:, :, cols].rearrange("p t (c i) -> p c t i", i=4),
                 pull[:, :, cols].rearrange("p t (c i) -> p c t i", i=4),
                 ALU.add,
             )
-            relaxed.append(woven)
+
+        for half in (LOW, HIGH):
+            make_pull(PACK - 1, half)
+        for q, cols in enumerate((FIRST, SECOND, THIRD, FOURTH)):
+            for pair in range(2):
+                bank = psum.tile([P, 2, QUARTER], F32, name="bank" + str(2 * q + pair))
+                for u in range(2):
+                    product(bank[:, u, :], w1_mx[2 * pair + u], x_word[:, cols], x_scale[:, cols])
+                for u in range(2):
+                    scale_y(2 * pair + u, cols, bank[:, u, :])
+            relax(relaxed[q // 2][:, (FIRST, SECOND)[q % 2], :], cols)
 
         idle = psum.tile([WARM, H], F32, name="bank7")
         for start in (0, P):

from contextlib import ExitStack

import concourse.mybir as mybir

K, T, S, H, N = 512, 2048, 512, 512, 512
FLOPS = 2 * K * H * S + 2 * H * N * S

F32 = mybir.dt.float32
BF16 = mybir.dt.bfloat16
I32 = mybir.dt.int32
U32 = mybir.dt.uint32
U16 = mybir.dt.uint16
U8 = mybir.dt.uint8
FP8X4 = mybir.dt.float8_e4m3fn_x4
ALU = mybir.AluOpType
ACT = mybir.ActivationFunctionType

P = 128
PACK = 4
HALF = 256
QUARTER = 128
WHOLE = slice(0, S)
LOW, HIGH = slice(0, HALF), slice(HALF, S)
FIRST, SECOND, THIRD, FOURTH = [slice(q * QUARTER, (q + 1) * QUARTER) for q in range(4)]
FRONT, BACK = slice(0, 2), slice(2, PACK)
TWO_SETS = 2 * P * PACK

W1_VECTOR = (192, 352)
W2_VECTOR = 256
WIDE = 704
OPENING = (slice(0, QUARTER), slice(QUARTER, HALF + QUARTER), FOURTH)
WARM = 32


def tile_picked_ylbm_str_po_kernel(
    tc, x_words, x_scales, w1, w2, eq, rate, offs, src, out_0, out_1, out_2
):
    nc = tc.nc
    with ExitStack() as ctx:
        sb = ctx.enter_context(tc.tile_pool(name="sb", bufs=1))
        psum = ctx.enter_context(tc.psum_pool(name="psum", bufs=1))

        def tile(shape, dtype, name, tag=None):
            return sb.tile(shape, dtype, name=name, tag=tag or name, align_bytes=64)

        def offsets(list_tile, cols):
            return list_tile[:, cols.start // 16 : cols.stop // 16]

        def quantize(codes, scales, values):
            nc.vector.quantize_mx(out=codes.bitcast(FP8X4), scales=scales, in_=values)

        def product(bank, stationary, codes, scales):
            nc.tensor.matmul_mx(
                out=bank,
                lhsT=stationary[0].bitcast(FP8X4),
                lhsT_scale=stationary[1],
                rhs=codes.bitcast(FP8X4),
                rhs_scale=scales,
                start=True,
                stop=True,
            )

        offs_sb = tile([P, S // 16], U16, "offs_sb")
        src_sb = tile([P, S // 16], U16, "src_sb")
        xs_table = tile([P, T], U8, "xs_table")
        xw_table = tile([P, T], I32, "xw_table")
        rate_sb = tile([P, PACK], F32, "rate_sb")
        keep_sb = tile([P, PACK], F32, "keep_sb")
        w1_raw = tile([P, PACK, H], F32, "w1_raw")
        x_scale = tile([P, S], U8, "x_scale")

        nc.vector.memset(xs_table[:].bitcast(I32), 0)
        nc.vector.memset(x_scale[:].bitcast(I32), 0)

        w1_rows = w1.rearrange("(p j) c -> p j c", j=PACK)
        nc.sync.dma_start(out=w1_raw[:, 0:1, :], in_=w1_rows[:, 0:1, :])
        nc.sync.dma_start(offs_sb[:], offs)
        nc.sync.dma_start(out=xs_table[0:P:8, :].bitcast(I32), in_=x_scales[0].bitcast(I32))
        nc.sync.dma_start(out=w1_raw[:, 1:2, :], in_=w1_rows[:, 1:2, :])
        nc.sync.dma_start(out=w1_raw[:, BACK, :], in_=w1_rows[:, BACK, :])
        nc.scalar.dma_start(out=rate_sb[:], in_=rate.rearrange("(p t) o -> p (t o)", t=PACK))
        nc.sync.dma_start(out=xw_table[:], in_=x_words[0].rearrange("p n t -> p (n t)").bitcast(I32))
        nc.scalar.activation(keep_sb[:], rate_sb[:], ACT.Copy, bias=1.0, scale=-1.0)

        xs_picked = tile([P, S], U8, "xs_picked")
        nc.vector.tensor_copy(xs_picked[:], xs_table[:].indirect(offs_sb[:]))
        for q in range(4):
            nc.sync.dma_start(
                out=x_scale[32 * q : 32 * q + 4, :].bitcast(I32),
                in_=xs_picked[32 * q : 32 * (q + 1) : 8, :].bitcast(I32),
            )

        late = tile([P, 2 * PACK * S], F32, "late", "xs_table")
        eq_raw = late[:, : PACK * S].rearrange("p (t c) -> p t c", t=PACK)
        w2_raw = late[:, PACK * S :].rearrange("p (j c) -> p j c", j=PACK)
        eq_rows = eq.rearrange("(p t) c -> p t c", t=PACK)
        for sets in (FRONT, slice(2, 3), slice(3, PACK)):
            nc.sync.dma_start(out=eq_raw[:, sets, :], in_=eq_rows[:, sets, :])
        w2_rows = w2.rearrange("(p j) c -> p j c", j=PACK)
        for rows in (FRONT, BACK):
            nc.sync.dma_start(out=w2_raw[:, rows, :], in_=w2_rows[:, rows, :])
        nc.sync.dma_start(src_sb[:], src)

        w1_grouped = tile([P, PACK, P, PACK], BF16, "w1_grouped")

        def deal_w1(copy, cols, rows):
            copy(
                out=w1_grouped[:, :, cols.start // PACK : cols.stop // PACK, rows].rearrange("p (u t) m j -> p u m t j", t=2),
                in_=w1_raw[:, rows, cols].rearrange("p j (m u t) -> p u m t j", u=2, t=2),
            )

        for rows, share in zip((FRONT, BACK), W1_VECTOR):
            deal_w1(nc.vector.tensor_copy, slice(0, share), rows)
            deal_w1(nc.scalar.copy, slice(share, H), rows)
        w1_codes = tile([P, H], I32, "w1_codes")
        w1_scales = tile([P, H], U8, "w1_scales")
        w1_mx = [(w1_codes[:, t * P : (t + 1) * P], w1_scales[:, t * P : (t + 1) * P]) for t in range(PACK)]
        for t in range(PACK):
            quantize(w1_mx[t][0], w1_mx[t][1], w1_grouped[:, t, :, :].rearrange("p m j -> p (m j)"))

        x_word = tile([P, S], I32, "x_word")
        for cols in (FIRST, SECOND, HIGH):
            nc.vector.tensor_copy(x_word[:, cols].bitcast(U32), xw_table[:].bitcast(U32).indirect(offsets(offs_sb, cols)))

        pull = tile([P, PACK, S], F32, "pull")

        def make_pull(t, cols):
            nc.vector.tensor_scalar(pull[:, t, cols], eq_raw[:, t, cols], rate_sb[:, t : t + 1], None, ALU.mult)

        for t in range(PACK - 1):
            make_pull(t, WHOLE)

        relaxed = [tile([P, HALF, PACK], BF16, "rr" + str(h)) for h in range(2)]
        kept = tile([P, PACK, S], F32, "kept")

        def scale_y(t, cols, bank):
            nc.scalar.activation(kept[:, t, cols], bank, ACT.Copy, scale=keep_sb[:, t : t + 1])

        def relax(woven, cols):
            nc.vector.tensor_tensor(
                woven.rearrange("p (c i) t -> p c t i", i=4),
                kept[:, :, cols].rearrange("p t (c i) -> p c t i", i=4),
                pull[:, :, cols].rearrange("p t (c i) -> p c t i", i=4),
                ALU.add,
            )

        for half in (LOW, HIGH):
            make_pull(PACK - 1, half)
        for q, cols in enumerate((FIRST, SECOND, THIRD, FOURTH)):
            for pair in range(2):
                bank = psum.tile([P, 2, QUARTER], F32, name="bank" + str(2 * q + pair))
                for u in range(2):
                    product(bank[:, u, :], w1_mx[2 * pair + u], x_word[:, cols], x_scale[:, cols])
                for u in range(2):
                    scale_y(2 * pair + u, cols, bank[:, u, :])
            relax(relaxed[q // 2][:, (FIRST, SECOND)[q % 2], :], cols)

        idle = psum.tile([WARM, H], F32, name="bank7")
        for start in (0, P):
            narrow = slice(start, start + WARM)
            product(idle[:], (w1_codes[:, narrow], w1_scales[:, narrow]), w1_codes[:], w1_scales[:])

        rr_codes = tile([P, S], I32, "rr_codes")
        rr_scales = tile([P, S], U8, "rr_scales")

        def quantize_rr(h, cols):
            quantize(rr_codes[:, cols], rr_scales[:, cols], relaxed[h][:].rearrange("p n t -> p (n t)"))

        w2_rounded = tile([P, 2 * TWO_SETS - W2_VECTOR], BF16, "w2_rounded", "x_word")
        w2_back = w2_rounded[:, :TWO_SETS].rearrange("p (t m j) -> p t m j", t=2, j=PACK)
        w2_front = w2_rounded[:, TWO_SETS - W2_VECTOR :].rearrange("p (t m j) -> p t m j", t=2, j=PACK)

        def deal_w2(copy, grouped, sets, cols, rows):
            copy(
                out=grouped[:, :, cols.start // PACK : cols.stop // PACK, rows].rearrange("p t m j -> p m t j"),
                in_=w2_raw[:, rows, cols].rearrange("p j (m t) -> p m t j", t=PACK)[:, :, sets, :],
            )

        def quantize_w2(grouped, t):
            codes = tile([P, P], I32, "w2_codes" + str(t))
            scales = tile([P, P], U8, "w2_scales" + str(t))
            quantize(codes[:], scales[:], grouped[:, t % 2, :, :].rearrange("p m j -> p (m j)"))
            return codes[:], scales[:]

        for rows in (FRONT, BACK):
            deal_w2(nc.scalar.copy, w2_front, FRONT, slice(0, N), rows)
        quantize_rr(0, LOW)
        product(idle[:], (rr_codes[:, :WARM], rr_scales[:, :WARM]), w1_codes[:], w1_scales[:])
        quantize_rr(1, HIGH)
        w2_mx = [quantize_w2(w2_front, t) for t in range(2)]
        deal_w2(nc.scalar.copy, w2_back, BACK, slice(0, N - W2_VECTOR), slice(0, PACK))
        deal_w2(nc.vector.tensor_copy, w2_back, BACK, slice(N - W2_VECTOR, N), slice(0, PACK))
        w2_mx.append(quantize_w2(w2_back, 2))

        f_rows = tile([P, PACK * S + WIDE - S], F32, "f_rows")
        nc.vector.memset(f_rows[:, PACK * S :], 0.0)

        def f_start(t):
            return (PACK - 1 - t) * S

        def populations(bank_number, t, cols, copy):
            bank = psum.tile([P, cols.stop - cols.start], F32, name="bank" + str(bank_number))
            product(bank[:], w2_mx[t], rr_codes[:, cols], rr_scales[:, cols])
            copy(out=f_rows[:, f_start(t) + cols.start : f_start(t) + cols.stop], in_=bank[:])

        for bank_number, copy in enumerate((nc.scalar.copy, nc.scalar.copy, nc.vector.tensor_copy)):
            populations(bank_number, 0, OPENING[bank_number], copy)
        w2_mx.append(quantize_w2(w2_back, 3))
        for t in range(1, PACK):
            populations(len(OPENING) - 1 + t, t, WHOLE, nc.scalar.copy)

        out_rows = out_0.rearrange("(p t) n -> p t n", t=PACK)
        out_words = out_1[0].rearrange("p n t -> p (n t)").bitcast(I32)
        out_codes = tile([P, S], I32, "out_codes")
        out_scales = tile([P, S], U8, "out_scales")
        streamed = tile([P, PACK, S], F32, "streamed")
        rounded = tile([P, S, PACK], BF16, "rounded")

        def gather_on_scalar(out, in_):
            nc.scalar.activation(out, in_, ACT.Copy)

        def round_on_gpsimd(out, in_):
            nc.gpsimd.tensor_scalar(out, in_, 1.0, 0.0, ALU.mult, ALU.add)

        def stream(gather, t, cols, window):
            gather(
                streamed[:, t, cols],
                f_rows[:, f_start(t) : f_start(t) + window].indirect(offsets(src_sb, cols)),
            )

        def store(sets):
            nc.sync.dma_start(out=out_rows[:, sets, :], in_=streamed[:, sets, :])

        def weave_pair(copy, sets, cols):
            copy(rounded[:, cols, sets], streamed[:, sets, cols].rearrange("p t c -> p c t"))

        def quantize_out(cols):
            quantize(out_codes[:, cols], out_scales[:, cols], rounded[:, cols, :].rearrange("p n t -> p (n t)"))

        def weave_all(copy, cols):
            copy(
                rounded[:, cols, :].rearrange("p (c i) t -> p c t i", i=4),
                streamed[:, :, cols].rearrange("p t (c i) -> p c t i", i=4),
            )

        stream(nc.vector.tensor_copy, 0, WHOLE, WIDE)
        store(slice(0, 1))
        for cols in (LOW, HIGH):
            stream(nc.vector.tensor_copy, 1, cols, S)
        store(slice(1, 2))
        weave_pair(round_on_gpsimd, FRONT, LOW)
        stream(gather_on_scalar, 2, THIRD, S)
        for cols in (LOW, FOURTH):
            stream(nc.vector.tensor_copy, 2, cols, S)
        store(slice(2, 3))
        for cols in (THIRD, FIRST, SECOND):
            stream(gather_on_scalar, 3, cols, S)
        stream(nc.vector.tensor_copy, 3, FOURTH, S)
        store(slice(3, PACK))
        weave_pair(round_on_gpsimd, slice(0, PACK), THIRD)
        weave_all(nc.vector.tensor_copy, FOURTH)
        for cols in (FIRST, SECOND):
            weave_pair(nc.scalar.copy, BACK, cols)
        for cols in (THIRD, FOURTH):
            quantize_out(cols)
        nc.sync.dma_start(out=out_words[:, HIGH], in_=out_codes[:, HIGH])
        for cols in (FIRST, SECOND):
            quantize_out(cols)
        nc.scalar.dma_start(out=out_words[:, LOW], in_=out_codes[:, LOW])
        for q in range(4):
            queue = nc.sync if q % 2 else nc.scalar
            queue.dma_start(
                out=out_2[0, 4 * q : 4 * q + 4, :].bitcast(I32),
                in_=out_scales[32 * q : 32 * q + 4, :].bitcast(I32),
            )
